import numpy as np
import ml_dtypes


def mxq(x, axis, fmt="e4m3"):
    dtype, down = {"e4m3": (ml_dtypes.float8_e4m3fn, 7), "e5m2": (ml_dtypes.float8_e5m2, 14)}[fmt]
    v = np.moveaxis(np.asarray(x, np.float32).astype(ml_dtypes.bfloat16).astype(np.float64), axis, -1)
    blocks = v.reshape(v.shape[:-1] + (-1, 32))
    amax = np.abs(blocks).max(-1, keepdims=True)
    byte = np.maximum(np.where(amax > 0, np.frexp(amax)[1] - 1 + 127, 0) - down, 1)
    scale = np.exp2(byte - 127.0)
    codes = (blocks / scale).astype(np.float32).astype(dtype).astype(np.float64)
    return np.moveaxis((codes * scale).reshape(v.shape), -1, axis)


WIDE = False


def mx_kscale(k):
    if not WIDE:
        return np.ones(k)
    levels = np.array([10, -10, 5, -5, 0])
    if k % 512:
        return np.exp2(np.random.permutation(np.resize(levels, k // 32))).repeat(32)
    a = np.empty((k // 512, 16))
    for p in range(k // 512):
        a[p, :8] = np.random.permutation(np.resize(levels, 8))
        for g in range(8):
            far = levels[np.abs(levels - a[p, g]) >= 10]
            a[p, g + 8] = far[np.random.randint(len(far))]
    return np.exp2(a.ravel()).repeat(32)


def f64(x):
    return np.asarray(x).astype(np.float64)


def striped(idx):
    return np.tile(idx.reshape(-1, 16).T, (8, 1)).astype(np.uint16)


def unstriped(offs):
    return offs[:16].T.reshape(-1).astype(np.int64)


def pack_weight(w):
    k, n = w.shape
    w = f64(np.asarray(w, np.float32).astype(ml_dtypes.bfloat16)).reshape(k // 32, 32, n)
    amax = np.abs(w).max(1)
    byte = np.clip(np.where(amax > 0, np.frexp(amax)[1] - 1 + 127 - 7, 1), 1, 254)
    scaled = (w * np.exp2(127.0 - byte)[:, None, :]).reshape(k, n).astype(np.float32)
    words = np.ascontiguousarray(scaled.reshape(k // 512, 128, 4, n).transpose(0, 1, 3, 2)).astype(ml_dtypes.float8_e4m3fn).view(np.uint8)
    return words, np.ascontiguousarray(byte.astype(np.uint8).reshape(k // 512, 16, n))


def unpack_weight(words, scales):
    g, p, n, _ = words.shape
    vals = np.ascontiguousarray(words).view(ml_dtypes.float8_e4m3fn).astype(np.float64) * np.repeat(np.exp2(scales.astype(np.float64) - 127.0), 8, axis=1)[..., None]
    return vals.transpose(0, 1, 3, 2).reshape(g * 512, n)


def relu(v):
    return np.maximum(v, 0.0)


K, T, S, H, N, R = 512, 2048, 512, 512, 256, 1024


def setup_inputs():
    n = np.random.standard_normal
    s = mx_kscale(K)[:, None]
    u = mx_kscale(H)
    packed_xT = pack_weight(n((K, T)) * s)
    return {
        "x_words": packed_xT[0],
        "x_scales": packed_xT[1],
        "w1": (n((K, H)) / np.sqrt(K) / s * u).astype(np.float32),
        "w2": (n((H, N)) / np.sqrt(H) / u[:, None]).astype(np.float32),
        "wide": (0.5 * n((N, R))).astype(np.float32),
        "offs": striped(np.random.permutation(T)[:S]),
        "cross1": striped(np.random.randint(0, R, S)),
        "cross2": striped(np.random.randint(0, R, S)),
        "cross3": striped(np.random.randint(0, R, S)),
    }


def reference(x_words, x_scales, w1, w2, wide, offs, cross1, cross2, cross3):
    xq = unpack_weight(x_words, x_scales)[:, unstriped(offs)]
    h = relu(mxq(f64(w1), 0, "e4m3").T @ xq)
    y = mxq(f64(w2), 0, "e4m3").T @ mxq(h, 0, "e4m3")
    return y + f64(wide)[:, unstriped(cross1)] + f64(wide)[:, unstriped(cross2)] + f64(wide)[:, unstriped(cross3)]

@@ -1,0 +1,131 @@
+from contextlib import ExitStack
+
+import concourse.mybir as mybir
+
+F32 = mybir.dt.float32
+BF16 = mybir.dt.bfloat16
+I32 = mybir.dt.int32
+U32 = mybir.dt.uint32
+U16 = mybir.dt.uint16
+U8 = mybir.dt.uint8
+FP8X4 = mybir.dt.float8_e4m3fn_x4
+ADD = mybir.AluOpType.add
+COPY = mybir.ActivationFunctionType.Copy
+RELU = mybir.ActivationFunctionType.Relu
+
+K, T, S, H, N, R = 512, 2048, 512, 512, 256, 1024
+P = 128
+PACK = 4
+CHUNK = 128
+FLOPS = 2 * K * H * S + 2 * H * N * S
+
+
+def tile_picked_ywide_none_p_kernel(tc, x_words, x_scales, w1, w2, wide, offs, cross1, cross2, cross3, out):
+    nc = tc.nc
+    with ExitStack() as ctx:
+        keep = ctx.enter_context(tc.tile_pool(name="keep", bufs=1))
+        psum = ctx.enter_context(tc.psum_pool(name="psum", bufs=1))
+
+        def load_list(src, name):
+            t = keep.tile([P, S // 16], U16, name=name)
+            nc.sync.dma_start(t[:], src)
+            return t
+
+        scale_table = keep.tile([P, T], U8, name="scale_table", align_bytes=64)
+        nc.vector.memset(scale_table[:].bitcast(I32), 0)
+
+        users = load_list(offs, "users")
+        wide_rows = [keep.tile([P, R], F32, name="wide%d" % b, align_bytes=64) for b in range(2)]
+        nc.sync.dma_start(wide_rows[0][:], wide[0:P, :])
+        for q in range(4):
+            nc.scalar.dma_start(scale_table[32 * q : 32 * q + 4, :].bitcast(I32), x_scales[0, 4 * q : 4 * q + 4, :].bitcast(I32))
+        crosses = [load_list(cross1, "c1")]
+        w1_raw = keep.tile([P, PACK, H], F32, name="w1_raw", align_bytes=64)
+        nc.sync.dma_start(w1_raw[:], w1.rearrange("(p j) c -> p j c", j=PACK))
+        crosses.append(load_list(cross2, "c2"))
+        crosses.append(load_list(cross3, "c3"))
+        word_table = keep.tile([P, T], I32, name="word_table", align_bytes=64)
+        nc.sync.dma_start(word_table[:], x_words[0].rearrange("p n t -> p (n t)").bitcast(I32))
+        w2_raw = keep.tile([P, PACK, N], F32, name="w2_raw", align_bytes=64)
+        nc.sync.dma_start(w2_raw[:], w2.rearrange("(p j) c -> p j c", j=PACK))
+        nc.sync.dma_start(wide_rows[1][:], wide[P : 2 * P, :])
+
+        x_sc = keep.tile([P, S], U8, name="x_sc", align_bytes=64)
+        nc.vector.tensor_copy(x_sc[:], scale_table[:].indirect(users[:]))
+
+        def wide_sum(b):
+            s1 = keep.tile([P, S], F32, name="s1_%d" % b, align_bytes=64)
+            s2 = keep.tile([P, S], F32, name="s2_%d" % b, align_bytes=64)
+            s3 = keep.tile([P, S], F32, name="s3_%d" % b, align_bytes=64)
+            nc.vector.tensor_copy(s1[:], wide_rows[b][:].indirect(crosses[0][:]))
+            nc.vector.tensor_tensor(s2[:], wide_rows[b][:].indirect(crosses[1][:]), s1[:], ADD)
+            nc.vector.tensor_tensor(s3[:], wide_rows[b][:].indirect(crosses[2][:]), s2[:], ADD)
+            return s3
+
+        sums = [wide_sum(0)]
+
+        w1_bf = keep.tile([P, H * PACK], BF16, name="w1_bf", align_bytes=64)
+        nc.scalar.activation(
+            w1_bf[:].rearrange("p (t m j) -> p m j t", t=PACK, j=PACK),
+            w1_raw[:].rearrange("p j (m t) -> p m j t", t=PACK),
+            COPY,
+        )
+        w2_bf = keep.tile([P, N * PACK], BF16, name="w2_bf", align_bytes=64)
+        nc.scalar.activation(
+            w2_bf[:].rearrange("p (c i j) -> p c j i", i=4, j=PACK),
+            w2_raw[:].rearrange("p j (c i) -> p c j i", i=4),
+            COPY,
+        )
+
+        x_codes = keep.tile([P, S], U32, name="x_codes", align_bytes=64)
+        nc.vector.tensor_copy(x_codes[:], word_table[:].bitcast(U32).indirect(users[:]))
+
+        w1_codes = keep.tile([P, H], U32, name="w1_codes", align_bytes=64)
+        w1_sc = keep.tile([P, H], U8, name="w1_sc", align_bytes=64)
+        nc.vector.quantize_mx(out=w1_codes[:].bitcast(FP8X4), scales=w1_sc[:], in_=w1_bf[:])
+        w2_codes = keep.tile([P, N], U32, name="w2_codes", align_bytes=64)
+        w2_sc = keep.tile([P, N], U8, name="w2_sc", align_bytes=64)
+        nc.vector.quantize_mx(out=w2_codes[:].bitcast(FP8X4), scales=w2_sc[:], in_=w2_bf[:])
+
+        h_bf = keep.tile([P, S * PACK], BF16, name="h_bf", align_bytes=64)
+        for c in range(S // CHUNK):
+            cols = slice(c * CHUNK, (c + 1) * CHUNK)
+            bank = psum.tile([P, PACK, CHUNK], F32, name="hbank%d" % c)
+            for t in range(PACK):
+                wc = slice(t * P, (t + 1) * P)
+                nc.tensor.matmul_mx(
+                    out=bank[:, t, :],
+                    lhsT=w1_codes[:, wc].bitcast(FP8X4),
+                    lhsT_scale=w1_sc[:, wc],
+                    rhs=x_codes[:, cols].bitcast(FP8X4),
+                    rhs_scale=x_sc[:, cols],
+                    start=True,
+                    stop=True,
+                )
+            nc.scalar.activation(
+                h_bf[:, c * CHUNK * PACK : (c + 1) * CHUNK * PACK].rearrange("p (n t) -> p n t", t=PACK),
+                bank[:].rearrange("p t n -> p n t"),
+                RELU,
+            )
+
+        sums.append(wide_sum(1))
+
+        h_codes = keep.tile([P, S], U32, name="h_codes", align_bytes=64)
+        h_sc = keep.tile([P, S], U8, name="h_sc", align_bytes=64)
+        nc.vector.quantize_mx(out=h_codes[:].bitcast(FP8X4), scales=h_sc[:], in_=h_bf[:])
+
+        for b in range(2):
+            rows = slice(b * P, (b + 1) * P)
+            ybank = psum.tile([P, S], F32, name="ybank%d" % b)
+            nc.tensor.matmul_mx(
+                out=ybank[:],
+                lhsT=w2_codes[:, rows].bitcast(FP8X4),
+                lhsT_scale=w2_sc[:, rows],
+                rhs=h_codes[:].bitcast(FP8X4),
+                rhs_scale=h_sc[:],
+                start=True,
+                stop=True,
+            )
+            res = keep.tile([P, S], F32, name="res%d" % b, align_bytes=64)
+            nc.vector.tensor_tensor(res[:], ybank[:], sums[b][:], ADD)
+            nc.sync.dma_start(out[rows, :], res[:])

@@ -1,6 +1,7 @@
 from contextlib import ExitStack
 
 import concourse.mybir as mybir
+from concourse.masks import make_identity
 
 F32 = mybir.dt.float32
 BF16 = mybir.dt.bfloat16
@@ -18,6 +19,7 @@ P = 128
 PACK = 4
 CHUNK = 128
 FLOPS = 2 * K * H * S + 2 * H * N * S
+HALF = S // 2
 
 
 def tile_picked_ywide_none_p_kernel(tc, x_words, x_scales, w1, w2, wide, offs, cross1, cross2, cross3, out):
@@ -33,63 +35,86 @@ def tile_picked_ywide_none_p_kernel(tc, x_words, x_scales, w1, w2, wide, offs, c
 
         scale_table = keep.tile([P, T], U8, name="scale_table", align_bytes=64)
         nc.vector.memset(scale_table[:].bitcast(I32), 0)
+        ident = keep.tile([P, P], F32, name="ident", align_bytes=64)
+        make_identity(nc, ident[:])
 
-        users = load_list(offs, "users")
         wide_rows = [keep.tile([P, R], F32, name="wide%d" % b, align_bytes=64) for b in range(2)]
         nc.sync.dma_start(wide_rows[0][:], wide[0:P, :])
-        for q in range(4):
-            nc.scalar.dma_start(scale_table[32 * q : 32 * q + 4, :].bitcast(I32), x_scales[0, 4 * q : 4 * q + 4, :].bitcast(I32))
-        crosses = [load_list(cross1, "c1")]
-        w1_raw = keep.tile([P, PACK, H], F32, name="w1_raw", align_bytes=64)
+        crosses = [load_list(cross1, "c1"), load_list(cross2, "c2"), load_list(cross3, "c3")]
+        w1_raw = keep.tile([P, PACK, H], F32, name="w1_raw", tag="w1_raw", align_bytes=64)
         nc.sync.dma_start(w1_raw[:], w1.rearrange("(p j) c -> p j c", j=PACK))
-        crosses.append(load_list(cross2, "c2"))
-        crosses.append(load_list(cross3, "c3"))
-        word_table = keep.tile([P, T], I32, name="word_table", align_bytes=64)
+        users = load_list(offs, "users")
+        for r in range(4):
+            nc.sync.dma_start(scale_table[r:P:32, :].bitcast(I32), x_scales[0, r:16:4, :].bitcast(I32))
+        word_table = keep.tile([P, T], I32, name="word_table", tag="word_table", align_bytes=64)
         nc.sync.dma_start(word_table[:], x_words[0].rearrange("p n t -> p (n t)").bitcast(I32))
-        w2_raw = keep.tile([P, PACK, N], F32, name="w2_raw", align_bytes=64)
-        nc.sync.dma_start(w2_raw[:], w2.rearrange("(p j) c -> p j c", j=PACK))
         nc.sync.dma_start(wide_rows[1][:], wide[P : 2 * P, :])
+        w2_raw = keep.tile([P, PACK, N], F32, name="w2_raw", tag="h_bf1", align_bytes=64)
+        nc.sync.dma_start(w2_raw[:], w2.rearrange("(p j) c -> p j c", j=PACK))
+
+        def look_up(b, i, first, count, so_far, tag):
+            s = keep.tile([P, count], F32, name="sum%d_%d_%d" % (b, i, first), tag=tag, align_bytes=64)
+            picked = wide_rows[b][:].indirect(crosses[i][:, first // 16 : (first + count) // 16])
+            if so_far is None:
+                nc.vector.tensor_copy(s[:], picked)
+            else:
+                nc.vector.tensor_tensor(s[:], picked, so_far[:], ADD)
+            return s
+
+        turned = psum.tile([P, S // P, P], F32, name="turned")
+        for i in range(3):
+            g = look_up(0, i, 0, S, None, "g%d" % i)
+            for c in range(S // P):
+                nc.tensor.matmul(
+                    turned[:, c, :],
+                    g[:, c * P : (c + 1) * P],
+                    ident[:],
+                    start=(i == 0 and c == 0),
+                    stop=(i == 2 and c == S // P - 1),
+                    is_transpose=True,
+                )
 
         x_sc = keep.tile([P, S], U8, name="x_sc", align_bytes=64)
         nc.vector.tensor_copy(x_sc[:], scale_table[:].indirect(users[:]))
 
-        def wide_sum(b):
-            s1 = keep.tile([P, S], F32, name="s1_%d" % b, align_bytes=64)
-            s2 = keep.tile([P, S], F32, name="s2_%d" % b, align_bytes=64)
-            s3 = keep.tile([P, S], F32, name="s3_%d" % b, align_bytes=64)
-            nc.vector.tensor_copy(s1[:], wide_rows[b][:].indirect(crosses[0][:]))
-            nc.vector.tensor_tensor(s2[:], wide_rows[b][:].indirect(crosses[1][:]), s1[:], ADD)
-            nc.vector.tensor_tensor(s3[:], wide_rows[b][:].indirect(crosses[2][:]), s2[:], ADD)
-            return s3
-
-        sums = [wide_sum(0)]
-
-        w1_bf = keep.tile([P, H * PACK], BF16, name="w1_bf", align_bytes=64)
+        w1_bf = keep.tile([P, H * PACK], BF16, name="w1_bf", tag="w1_bf", align_bytes=64)
         nc.scalar.activation(
             w1_bf[:].rearrange("p (t m j) -> p m j t", t=PACK, j=PACK),
             w1_raw[:].rearrange("p j (m t) -> p m j t", t=PACK),
             COPY,
         )
-        w2_bf = keep.tile([P, N * PACK], BF16, name="w2_bf", align_bytes=64)
+
+        turned_sb = keep.tile([P, S // P, P], F32, name="turned_sb", tag="w1_raw", align_bytes=64)
+        nc.scalar.copy(turned_sb[:], turned[:])
+        back = psum.tile([P, S // P, P], F32, name="back")
+        for c in range(S // P):
+            nc.tensor.transpose(back[:, c, :], turned_sb[:, c, :], ident[:])
+        sum0 = keep.tile([P, S], F32, name="sum0", align_bytes=64)
+        nc.scalar.copy(sum0[:], back[:].rearrange("p c n -> p (c n)"))
+
+        w1_codes = keep.tile([P, H], U32, name="w1_codes", align_bytes=64)
+        w1_sc = keep.tile([P, H], U8, name="w1_sc", align_bytes=64)
+        nc.vector.quantize_mx(out=w1_codes[:].bitcast(FP8X4), scales=w1_sc[:], in_=w1_bf[:])
+
+        x_codes = []
+        for u in range(2):
+            xc = keep.tile([P, HALF], U32, name="x_codes%d" % u, tag=("w1_bf", "x_codes1")[u], align_bytes=64)
+            nc.vector.tensor_copy(xc[:], word_table[:].bitcast(U32).indirect(users[:, u * HALF // 16 : (u + 1) * HALF // 16]))
+            x_codes.append(xc)
+
+        sum1 = [look_up(1, 0, u * HALF, HALF, None, ("word_table", "s10b")[u]) for u in range(2)]
+        sum1 = [look_up(1, 1, u * HALF, HALF, sum1[u], "s11_%d" % u) for u in range(2)]
+
+        w2_bf = keep.tile([P, N * PACK], BF16, name="w2_bf", tag="w2_bf", align_bytes=64)
         nc.scalar.activation(
             w2_bf[:].rearrange("p (c i j) -> p c j i", i=4, j=PACK),
             w2_raw[:].rearrange("p j (c i) -> p c j i", i=4),
             COPY,
         )
 
-        x_codes = keep.tile([P, S], U32, name="x_codes", align_bytes=64)
-        nc.vector.tensor_copy(x_codes[:], word_table[:].bitcast(U32).indirect(users[:]))
-
-        w1_codes = keep.tile([P, H], U32, name="w1_codes", align_bytes=64)
-        w1_sc = keep.tile([P, H], U8, name="w1_sc", align_bytes=64)
-        nc.vector.quantize_mx(out=w1_codes[:].bitcast(FP8X4), scales=w1_sc[:], in_=w1_bf[:])
-        w2_codes = keep.tile([P, N], U32, name="w2_codes", align_bytes=64)
-        w2_sc = keep.tile([P, N], U8, name="w2_sc", align_bytes=64)
-        nc.vector.quantize_mx(out=w2_codes[:].bitcast(FP8X4), scales=w2_sc[:], in_=w2_bf[:])
-
-        h_bf = keep.tile([P, S * PACK], BF16, name="h_bf", align_bytes=64)
+        h_bf = [keep.tile([P, HALF * PACK], BF16, name="h_bf%d" % u, tag="h_bf%d" % u, align_bytes=64) for u in range(2)]
         for c in range(S // CHUNK):
-            cols = slice(c * CHUNK, (c + 1) * CHUNK)
+            u, e = divmod(c, 2)
             bank = psum.tile([P, PACK, CHUNK], F32, name="hbank%d" % c)
             for t in range(PACK):
                 wc = slice(t * P, (t + 1) * P)
@@ -97,35 +122,50 @@ def tile_picked_ywide_none_p_kernel(tc, x_words, x_scales, w1, w2, wide, offs, c
                     out=bank[:, t, :],
                     lhsT=w1_codes[:, wc].bitcast(FP8X4),
                     lhsT_scale=w1_sc[:, wc],
-                    rhs=x_codes[:, cols].bitcast(FP8X4),
-                    rhs_scale=x_sc[:, cols],
+                    rhs=x_codes[u][:, e * CHUNK : (e + 1) * CHUNK].bitcast(FP8X4),
+                    rhs_scale=x_sc[:, c * CHUNK : (c + 1) * CHUNK],
                     start=True,
                     stop=True,
                 )
             nc.scalar.activation(
-                h_bf[:, c * CHUNK * PACK : (c + 1) * CHUNK * PACK].rearrange("p (n t) -> p n t", t=PACK),
+                h_bf[u][:, e * CHUNK * PACK : (e + 1) * CHUNK * PACK].rearrange("p (n t) -> p n t", t=PACK),
                 bank[:].rearrange("p t n -> p n t"),
                 RELU,
             )
 
-        sums.append(wide_sum(1))
+        def quantise_h(u, tag):
+            codes = keep.tile([P, HALF], U32, name="h_codes%d" % u, tag=tag, align_bytes=64)
+            scales = keep.tile([P, HALF], U8, name="h_sc%d" % u, align_bytes=64)
+            nc.vector.quantize_mx(out=codes[:].bitcast(FP8X4), scales=scales[:], in_=h_bf[u][:])
+            return codes, scales
 
-        h_codes = keep.tile([P, S], U32, name="h_codes", align_bytes=64)
-        h_sc = keep.tile([P, S], U8, name="h_sc", align_bytes=64)
-        nc.vector.quantize_mx(out=h_codes[:].bitcast(FP8X4), scales=h_sc[:], in_=h_bf[:])
+        h_mx = [quantise_h(0, "h_codes0")]
 
-        for b in range(2):
-            rows = slice(b * P, (b + 1) * P)
-            ybank = psum.tile([P, S], F32, name="ybank%d" % b)
-            nc.tensor.matmul_mx(
-                out=ybank[:],
-                lhsT=w2_codes[:, rows].bitcast(FP8X4),
-                lhsT_scale=w2_sc[:, rows],
-                rhs=h_codes[:].bitcast(FP8X4),
-                rhs_scale=h_sc[:],
-                start=True,
-                stop=True,
-            )
-            res = keep.tile([P, S], F32, name="res%d" % b, align_bytes=64)
-            nc.vector.tensor_tensor(res[:], ybank[:], sums[b][:], ADD)
-            nc.sync.dma_start(out[rows, :], res[:])
+        w2_codes = keep.tile([P, N], U32, name="w2_codes", align_bytes=64)
+        w2_sc = keep.tile([P, N], U8, name="w2_sc", align_bytes=64)
+        nc.vector.quantize_mx(out=w2_codes[:].bitcast(FP8X4), scales=w2_sc[:], in_=w2_bf[:])
+
+        sum1[0] = look_up(1, 2, 0, HALF, sum1[0], "w2_bf")
+        h_mx.append(quantise_h(1, "s11_0"))
+        sum1[1] = look_up(1, 2, HALF, HALF, sum1[1], "h_bf1")
+
+        ybank = [psum.tile([P, 2, HALF], F32, name="ybank%d" % u) for u in range(2)]
+        for u in range(2):
+            for b in range(2):
+                rows = slice(b * P, (b + 1) * P)
+                nc.tensor.matmul_mx(
+                    out=ybank[u][:, b, :],
+                    lhsT=w2_codes[:, rows].bitcast(FP8X4),
+                    lhsT_scale=w2_sc[:, rows],
+                    rhs=h_mx[u][0][:].bitcast(FP8X4),
+                    rhs_scale=h_mx[u][1][:],
+                    start=True,
+                    stop=True,
+                )
+
+        for u in range(2):
+            cols = slice(u * HALF, (u + 1) * HALF)
+            for b, part in enumerate((sum0[:, cols], sum1[u][:])):
+                res = keep.tile([P, HALF], F32, name="res%d_%d" % (b, u), align_bytes=64)
+                nc.vector.tensor_tensor(res[:], ybank[u][:, b, :], part, ADD)
+                nc.sync.dma_start(out[b * P : (b + 1) * P, cols], res[:])

@@ -41,8 +41,11 @@ def tile_picked_ywide_none_p_kernel(tc, x_words, x_scales, w1, w2, wide, offs, c
         wide_rows = [keep.tile([P, R], F32, name="wide%d" % b, align_bytes=64) for b in range(2)]
         nc.sync.dma_start(wide_rows[0][:], wide[0:P, :])
         crosses = [load_list(cross1, "c1"), load_list(cross2, "c2"), load_list(cross3, "c3")]
-        w1_raw = keep.tile([P, PACK, H], F32, name="w1_raw", tag="w1_raw", align_bytes=64)
-        nc.sync.dma_start(w1_raw[:], w1.rearrange("(p j) c -> p j c", j=PACK))
+        w1_raw = []
+        for u in range(2):
+            raw = keep.tile([P, PACK, H // 2], F32, name="w1_raw%d" % u, tag="w1_raw%d" % u, align_bytes=64)
+            nc.sync.dma_start(raw[:], w1.rearrange("(p j) c -> p j c", j=PACK)[:, :, u * H // 2 : (u + 1) * H // 2])
+            w1_raw.append(raw)
         users = load_list(offs, "users")
         for r in range(4):
             nc.sync.dma_start(scale_table[r:P:32, :].bitcast(I32), x_scales[0, r:16:4, :].bitcast(I32))
@@ -78,13 +81,14 @@ def tile_picked_ywide_none_p_kernel(tc, x_words, x_scales, w1, w2, wide, offs, c
         nc.vector.tensor_copy(x_sc[:], scale_table[:].indirect(users[:]))
 
         w1_bf = keep.tile([P, H * PACK], BF16, name="w1_bf", tag="w1_bf", align_bytes=64)
-        nc.scalar.activation(
-            w1_bf[:].rearrange("p (t m j) -> p m j t", t=PACK, j=PACK),
-            w1_raw[:].rearrange("p j (m t) -> p m j t", t=PACK),
-            COPY,
-        )
+        for u in range(2):
+            nc.scalar.activation(
+                w1_bf[:].rearrange("p (t m j) -> p m j t", t=PACK, j=PACK)[:, u * P // 2 : (u + 1) * P // 2],
+                w1_raw[u][:].rearrange("p j (m t) -> p m j t", t=PACK),
+                COPY,
+            )
 
-        turned_sb = keep.tile([P, S // P, P], F32, name="turned_sb", tag="w1_raw", align_bytes=64)
+        turned_sb = keep.tile([P, S // P, P], F32, name="turned_sb", tag="w1_raw1", align_bytes=64)
         nc.scalar.copy(turned_sb[:], turned[:])
         back = psum.tile([P, S // P, P], F32, name="back")
         for c in range(S // P):

@@ -26,47 +26,52 @@ def tile_picked_ywide_none_p_kernel(tc, x_words, x_scales, w1, w2, wide, offs, c
     nc = tc.nc
     with ExitStack() as ctx:
         keep = ctx.enter_context(tc.tile_pool(name="keep", bufs=1))
+        reuse = ctx.enter_context(tc.tile_pool(name="reuse", bufs=1))
+        reuse1 = ctx.enter_context(tc.tile_pool(name="reuse1", bufs=1))
         psum = ctx.enter_context(tc.psum_pool(name="psum", bufs=1))
+
+        def sb(shape, dtype, name):
+            return keep.tile(shape, dtype, name=name, align_bytes=64)
 
         def load_list(src, name):
             t = keep.tile([P, S // 16], U16, name=name)
             nc.sync.dma_start(t[:], src)
             return t
 
-        scale_table = keep.tile([P, T], U8, name="scale_table", align_bytes=64)
+        scale_table = sb([P, T], U8, "scale_table")
         nc.vector.memset(scale_table[:].bitcast(I32), 0)
-        ident = keep.tile([P, P], F32, name="ident", align_bytes=64)
+        ident = sb([P, P], F32, "ident")
         make_identity(nc, ident[:])
 
-        wide_rows = [keep.tile([P, R], F32, name="wide%d" % b, align_bytes=64) for b in range(2)]
+        wide_rows = [sb([P, R], F32, "wide%d" % b) for b in range(2)]
         nc.sync.dma_start(wide_rows[0][:], wide[0:P, :])
         crosses = [load_list(cross1, "c1"), load_list(cross2, "c2"), load_list(cross3, "c3")]
-        w1_raw = []
-        for u in range(2):
-            raw = keep.tile([P, PACK, H // 2], F32, name="w1_raw%d" % u, tag="w1_raw%d" % u, align_bytes=64)
-            nc.sync.dma_start(raw[:], w1.rearrange("(p j) c -> p j c", j=PACK)[:, :, u * H // 2 : (u + 1) * H // 2])
-            w1_raw.append(raw)
+        w1_raw = [sb([P, PACK, H // 2], F32, "w1_raw0"), reuse1.tile([P, PACK, H // 2], F32, name="w1_raw1", align_bytes=64, offset=0)]
+        w1_view = w1.rearrange("(p j) c -> p j c", j=PACK)
+        nc.sync.dma_start(w1_raw[0][:], w1_view[:, :, 0 : H // 2])
+        nc.sync.dma_start(w1_raw[1][:], w1_view[:, :, H // 2 : H])
         users = load_list(offs, "users")
+        word_table = sb([P, T], I32, "word_table")
+        nc.sync.dma_start(word_table[:], x_words[0].rearrange("p n t -> p (n t)").bitcast(I32))
         for r in range(4):
             nc.sync.dma_start(scale_table[r:P:32, :].bitcast(I32), x_scales[0, r:16:4, :].bitcast(I32))
-        word_table = keep.tile([P, T], I32, name="word_table", tag="word_table", align_bytes=64)
-        nc.sync.dma_start(word_table[:], x_words[0].rearrange("p n t -> p (n t)").bitcast(I32))
-        nc.sync.dma_start(wide_rows[1][:], wide[P : 2 * P, :])
-        w2_raw = keep.tile([P, PACK, N], F32, name="w2_raw", tag="h_bf1", align_bytes=64)
+        w2_raw = reuse.tile([P, PACK, N], F32, name="w2_raw", align_bytes=64, offset=0)
         nc.sync.dma_start(w2_raw[:], w2.rearrange("(p j) c -> p j c", j=PACK))
+        nc.sync.dma_start(wide_rows[1][:], wide[P : 2 * P, :])
 
-        def look_up(b, i, first, count, so_far, tag):
-            s = keep.tile([P, count], F32, name="sum%d_%d_%d" % (b, i, first), tag=tag, align_bytes=64)
-            picked = wide_rows[b][:].indirect(crosses[i][:, first // 16 : (first + count) // 16])
-            if so_far is None:
-                nc.vector.tensor_copy(s[:], picked)
-            else:
-                nc.vector.tensor_tensor(s[:], picked, so_far[:], ADD)
-            return s
+        second = [sb([P, HALF], F32, "second%d" % u) for u in range(2)]
+        for u in range(2):
+            nc.gpsimd.memset(second[u][:, 0:1], 0.0)
+        zeros = [0.0, second[0][:, 0:1], 0.0, second[1][:, 0:1]]
+
+        def picked(b, i, first, count):
+            return wide_rows[b][:].indirect(crosses[i][:, first // 16 : (first + count) // 16])
 
         turned = psum.tile([P, S // P, P], F32, name="turned")
-        for i in range(3):
-            g = look_up(0, i, 0, S, None, "g%d" % i)
+
+        def turn_in(i):
+            g = sb([P, S], F32, "g%d" % i)
+            nc.vector.tensor_copy(g[:], picked(0, i, 0, S))
             for c in range(S // P):
                 nc.tensor.matmul(
                     turned[:, c, :],
@@ -77,10 +82,11 @@ def tile_picked_ywide_none_p_kernel(tc, x_words, x_scales, w1, w2, wide, offs, c
                     is_transpose=True,
                 )
 
-        x_sc = keep.tile([P, S], U8, name="x_sc", align_bytes=64)
-        nc.vector.tensor_copy(x_sc[:], scale_table[:].indirect(users[:]))
+        turn_in(0)
+        turn_in(1)
+        turn_in(2)
 
-        w1_bf = keep.tile([P, H * PACK], BF16, name="w1_bf", tag="w1_bf", align_bytes=64)
+        w1_bf = sb([P, H * PACK], BF16, "w1_bf")
         for u in range(2):
             nc.scalar.activation(
                 w1_bf[:].rearrange("p (t m j) -> p m j t", t=PACK, j=PACK)[:, u * P // 2 : (u + 1) * P // 2],
@@ -88,88 +94,97 @@ def tile_picked_ywide_none_p_kernel(tc, x_words, x_scales, w1, w2, wide, offs, c
                 COPY,
             )
 
-        turned_sb = keep.tile([P, S // P, P], F32, name="turned_sb", tag="w1_raw1", align_bytes=64)
-        nc.scalar.copy(turned_sb[:], turned[:])
-        back = psum.tile([P, S // P, P], F32, name="back")
-        for c in range(S // P):
-            nc.tensor.transpose(back[:, c, :], turned_sb[:, c, :], ident[:])
-        sum0 = keep.tile([P, S], F32, name="sum0", align_bytes=64)
-        nc.scalar.copy(sum0[:], back[:].rearrange("p c n -> p (c n)"))
+        def quantise(src, width, name):
+            codes = sb([P, width], U32, name + "_codes")
+            scales = sb([P, width], U8, name + "_sc")
+            nc.vector.quantize_mx(out=codes[:].bitcast(FP8X4), scales=scales[:], in_=src[:])
+            return codes, scales
 
-        w1_codes = keep.tile([P, H], U32, name="w1_codes", align_bytes=64)
-        w1_sc = keep.tile([P, H], U8, name="w1_sc", align_bytes=64)
-        nc.vector.quantize_mx(out=w1_codes[:].bitcast(FP8X4), scales=w1_sc[:], in_=w1_bf[:])
+        def product(dst, lhs, lcols, rhs, rcols):
+            nc.tensor.matmul_mx(
+                out=dst,
+                lhsT=lhs[0][:, lcols].bitcast(FP8X4),
+                lhsT_scale=lhs[1][:, lcols],
+                rhs=rhs[0][:, rcols].bitcast(FP8X4),
+                rhs_scale=rhs[1][:, rcols],
+                start=True,
+                stop=True,
+            )
 
-        x_codes = []
+        w1_mx = quantise(w1_bf, H, "w1")
+
+        turned_sb = reuse1.tile([P, S], F32, name="turned_sb", align_bytes=64, offset=5 * S)
+        nc.scalar.copy(turned_sb[:], turned[:].rearrange("p c n -> p (c n)"))
+
+        x_codes = reuse1.tile([P, S], U32, name="x_codes", align_bytes=64, offset=0)
+        nc.vector.tensor_copy(x_codes[:], word_table[:].bitcast(U32).indirect(users[:]))
+        x_sc = reuse1.tile([P, S], U8, name="x_sc", align_bytes=64, offset=4 * S)
         for u in range(2):
-            xc = keep.tile([P, HALF], U32, name="x_codes%d" % u, tag=("w1_bf", "x_codes1")[u], align_bytes=64)
-            nc.vector.tensor_copy(xc[:], word_table[:].bitcast(U32).indirect(users[:, u * HALF // 16 : (u + 1) * HALF // 16]))
-            x_codes.append(xc)
+            nc.vector.tensor_copy(
+                x_sc[:, u * HALF : (u + 1) * HALF],
+                scale_table[:].indirect(users[:, u * HALF // 16 : (u + 1) * HALF // 16]),
+            )
 
-        sum1 = [look_up(1, 0, u * HALF, HALF, None, ("word_table", "s10b")[u]) for u in range(2)]
-        sum1 = [look_up(1, 1, u * HALF, HALF, sum1[u], "s11_%d" % u) for u in range(2)]
-
-        w2_bf = keep.tile([P, N * PACK], BF16, name="w2_bf", tag="w2_bf", align_bytes=64)
+        w2_bf = sb([P, N * PACK], BF16, "w2_bf")
         nc.scalar.activation(
             w2_bf[:].rearrange("p (c i j) -> p c j i", i=4, j=PACK),
             w2_raw[:].rearrange("p j (c i) -> p c j i", i=4),
             COPY,
         )
 
-        h_bf = [keep.tile([P, HALF * PACK], BF16, name="h_bf%d" % u, tag="h_bf%d" % u, align_bytes=64) for u in range(2)]
+        h_bf = [
+            reuse.tile([P, HALF * PACK], BF16, name="h_bf0", align_bytes=64, offset=0),
+            reuse.tile([P, HALF * PACK], BF16, name="h_bf1", tag="h_bf1", align_bytes=64, offset=2 * HALF * PACK),
+        ]
         for c in range(S // CHUNK):
             u, e = divmod(c, 2)
-            bank = psum.tile([P, PACK, CHUNK], F32, name="hbank%d" % c)
+            bank = psum.tile([P, PACK, CHUNK], F32, name="hbank%d" % c, tag="bank%d" % c)
             for t in range(PACK):
-                wc = slice(t * P, (t + 1) * P)
-                nc.tensor.matmul_mx(
-                    out=bank[:, t, :],
-                    lhsT=w1_codes[:, wc].bitcast(FP8X4),
-                    lhsT_scale=w1_sc[:, wc],
-                    rhs=x_codes[u][:, e * CHUNK : (e + 1) * CHUNK].bitcast(FP8X4),
-                    rhs_scale=x_sc[:, c * CHUNK : (c + 1) * CHUNK],
-                    start=True,
-                    stop=True,
-                )
+                product(bank[:, t, :], w1_mx, slice(t * P, (t + 1) * P), (x_codes, x_sc), slice(c * CHUNK, (c + 1) * CHUNK))
             nc.scalar.activation(
                 h_bf[u][:, e * CHUNK * PACK : (e + 1) * CHUNK * PACK].rearrange("p (n t) -> p n t", t=PACK),
                 bank[:].rearrange("p t n -> p n t"),
                 RELU,
+                bias=zeros[c],
             )
 
-        def quantise_h(u, tag):
-            codes = keep.tile([P, HALF], U32, name="h_codes%d" % u, tag=tag, align_bytes=64)
-            scales = keep.tile([P, HALF], U8, name="h_sc%d" % u, align_bytes=64)
-            nc.vector.quantize_mx(out=codes[:].bitcast(FP8X4), scales=scales[:], in_=h_bf[u][:])
-            return codes, scales
+        w2_mx = quantise(w2_bf, N, "w2")
+        first = sb([P, S], F32, "first")
+        nc.vector.tensor_copy(first[:], picked(1, 0, 0, S))
 
-        h_mx = [quantise_h(0, "h_codes0")]
 
-        w2_codes = keep.tile([P, N], U32, name="w2_codes", align_bytes=64)
-        w2_sc = keep.tile([P, N], U8, name="w2_sc", align_bytes=64)
-        nc.vector.quantize_mx(out=w2_codes[:].bitcast(FP8X4), scales=w2_sc[:], in_=w2_bf[:])
-
-        sum1[0] = look_up(1, 2, 0, HALF, sum1[0], "w2_bf")
-        h_mx.append(quantise_h(1, "s11_0"))
-        sum1[1] = look_up(1, 2, HALF, HALF, sum1[1], "h_bf1")
-
-        ybank = [psum.tile([P, 2, HALF], F32, name="ybank%d" % u) for u in range(2)]
+        h_mx = []
+        y1 = []
+        y0_sb = []
         for u in range(2):
-            for b in range(2):
-                rows = slice(b * P, (b + 1) * P)
-                nc.tensor.matmul_mx(
-                    out=ybank[u][:, b, :],
-                    lhsT=w2_codes[:, rows].bitcast(FP8X4),
-                    lhsT_scale=w2_sc[:, rows],
-                    rhs=h_mx[u][0][:].bitcast(FP8X4),
-                    rhs_scale=h_mx[u][1][:],
-                    start=True,
-                    stop=True,
-                )
+            h_mx.append(quantise(h_bf[u], HALF, "h%d" % u))
+            yt = psum.tile([P, 2, P], F32, name="y0_%d" % u)
+            for e in range(2):
+                product(yt[:, e, :], h_mx[u], slice(e * P, (e + 1) * P), w2_mx, slice(0, P))
+            yb = psum.tile([P, HALF], F32, name="y1_%d" % u, tag="bank%d" % (2 * u))
+            product(yb[:], w2_mx, slice(P, 2 * P), h_mx[u], slice(0, HALF))
+            y1.append(yb)
+            ys = sb([P, HALF], F32, "y0_sb%d" % u)
+            nc.scalar.copy(ys[:], yt[:].rearrange("p e n -> p (e n)"))
+            y0_sb.append(ys)
+            nc.vector.tensor_tensor(second[u][:], picked(1, 1, u * HALF, HALF), first[:, u * HALF : (u + 1) * HALF], ADD)
+
+        third = [reuse.tile([P, HALF], F32, name="third0", tag="h_bf1", align_bytes=64, offset=2 * HALF * PACK), sb([P, HALF], F32, "third1")]
+        for u in range(2):
+            nc.vector.tensor_tensor(third[u][:], y1[u][:], second[u][:], ADD)
+        for u in range(2):
+            res = sb([P, HALF], F32, "res1_%d" % u)
+            nc.vector.tensor_tensor(res[:], picked(1, 2, u * HALF, HALF), third[u][:], ADD)
+            nc.sync.dma_start(out[P : 2 * P, u * HALF : (u + 1) * HALF], res[:])
 
         for u in range(2):
-            cols = slice(u * HALF, (u + 1) * HALF)
-            for b, part in enumerate((sum0[:, cols], sum1[u][:])):
-                res = keep.tile([P, HALF], F32, name="res%d_%d" % (b, u), align_bytes=64)
-                nc.vector.tensor_tensor(res[:], ybank[u][:, b, :], part, ADD)
-                nc.sync.dma_start(out[b * P : (b + 1) * P, cols], res[:])
+            back = psum.tile([P, 2, P], F32, name="back%d" % u, tag="bank%d" % (2 * u + 1))
+            for k, src in enumerate((turned_sb[:, u * HALF : (u + 1) * HALF], y0_sb[u][:])):
+                for e in range(2):
+                    nc.tensor.matmul(
+                        back[:, e, :], src[:, e * P : (e + 1) * P], ident[:],
+                        start=(k == 0 and e == 0), stop=(k == 1 and e == 1), is_transpose=True,
+                    )
+            res = sb([P, HALF], F32, "res0_%d" % u)
+            nc.scalar.copy(res[:], back[:].rearrange("p e n -> p (e n)"))
+            nc.scalar.dma_start(out[0:P, u * HALF : (u + 1) * HALF], res[:])

@@ -51,10 +51,10 @@ def tile_picked_ywide_none_p_kernel(tc, x_words, x_scales, w1, w2, wide, offs, c
         nc.sync.dma_start(w1_raw[0][:], w1_view[:, :, 0 : H // 2])
         nc.sync.dma_start(w1_raw[1][:], w1_view[:, :, H // 2 : H])
         users = load_list(offs, "users")
-        word_table = sb([P, T], I32, "word_table")
-        nc.sync.dma_start(word_table[:], x_words[0].rearrange("p n t -> p (n t)").bitcast(I32))
         for r in range(4):
             nc.sync.dma_start(scale_table[r:P:32, :].bitcast(I32), x_scales[0, r:16:4, :].bitcast(I32))
+        word_table = sb([P, T], I32, "word_table")
+        nc.sync.dma_start(word_table[:], x_words[0].rearrange("p n t -> p (n t)").bitcast(I32))
         w2_raw = reuse.tile([P, PACK, N], F32, name="w2_raw", align_bytes=64, offset=0)
         nc.sync.dma_start(w2_raw[:], w2.rearrange("(p j) c -> p j c", j=PACK))
         nc.sync.dma_start(wide_rows[1][:], wide[P : 2 * P, :])
@@ -85,6 +85,8 @@ def tile_picked_ywide_none_p_kernel(tc, x_words, x_scales, w1, w2, wide, offs, c
         turn_in(0)
         turn_in(1)
         turn_in(2)
+        x_sc = sb([P, S], U8, "x_sc")
+        nc.vector.tensor_copy(x_sc[:], scale_table[:].indirect(users[:]))
 
         w1_bf = sb([P, H * PACK], BF16, "w1_bf")
         for u in range(2):
@@ -117,20 +119,17 @@ def tile_picked_ywide_none_p_kernel(tc, x_words, x_scales, w1, w2, wide, offs, c
         nc.scalar.copy(turned_sb[:], turned[:].rearrange("p c n -> p (c n)"))
 
         x_codes = reuse1.tile([P, S], U32, name="x_codes", align_bytes=64, offset=0)
-        nc.vector.tensor_copy(x_codes[:], word_table[:].bitcast(U32).indirect(users[:]))
-        x_sc = reuse1.tile([P, S], U8, name="x_sc", align_bytes=64, offset=4 * S)
         for u in range(2):
             nc.vector.tensor_copy(
-                x_sc[:, u * HALF : (u + 1) * HALF],
-                scale_table[:].indirect(users[:, u * HALF // 16 : (u + 1) * HALF // 16]),
+                x_codes[:, u * HALF : (u + 1) * HALF],
+                word_table[:].bitcast(U32).indirect(users[:, u * HALF // 16 : (u + 1) * HALF // 16]),
             )
 
         w2_bf = sb([P, N * PACK], BF16, "w2_bf")
-        nc.scalar.activation(
-            w2_bf[:].rearrange("p (c i j) -> p c j i", i=4, j=PACK),
-            w2_raw[:].rearrange("p j (c i) -> p c j i", i=4),
-            COPY,
-        )
+        w2_dst = w2_bf[:].rearrange("p (c i j) -> p c j i", i=4, j=PACK)
+        w2_src = w2_raw[:].rearrange("p j (c i) -> p c j i", i=4)
+        nc.scalar.activation(w2_dst[:, 0:32], w2_src[:, 0:32], COPY)
+        nc.vector.tensor_copy(w2_dst[:, 32:64], w2_src[:, 32:64])
 
         h_bf = [
             reuse.tile([P, HALF * PACK], BF16, name="h_bf0", align_bytes=64, offset=0),
@@ -172,10 +171,11 @@ def tile_picked_ywide_none_p_kernel(tc, x_words, x_scales, w1, w2, wide, offs, c
         third = [reuse.tile([P, HALF], F32, name="third0", tag="h_bf1", align_bytes=64, offset=2 * HALF * PACK), sb([P, HALF], F32, "third1")]
         for u in range(2):
             nc.vector.tensor_tensor(third[u][:], y1[u][:], second[u][:], ADD)
-        for u in range(2):
-            res = sb([P, HALF], F32, "res1_%d" % u)
-            nc.vector.tensor_tensor(res[:], picked(1, 2, u * HALF, HALF), third[u][:], ADD)
-            nc.sync.dma_start(out[P : 2 * P, u * HALF : (u + 1) * HALF], res[:])
+        for lo, hi in ((0, HALF), (HALF, HALF + P), (HALF + P, S)):
+            res = sb([P, hi - lo], F32, "res1_%d" % lo)
+            u = lo // HALF
+            nc.vector.tensor_tensor(res[:], picked(1, 2, lo, hi - lo), third[u][:, lo - u * HALF : hi - u * HALF], ADD)
+            nc.sync.dma_start(out[P : 2 * P, lo:hi], res[:])
 
         for u in range(2):
             back = psum.tile([P, 2, P], F32, name="back%d" % u, tag="bank%d" % (2 * u + 1))

@@ -38,23 +38,30 @@ def tile_picked_ywide_none_p_kernel(tc, x_words, x_scales, w1, w2, wide, offs, c
             nc.sync.dma_start(t[:], src)
             return t
 
-        scale_table = sb([P, T], U8, "scale_table")
-        nc.vector.memset(scale_table[:].bitcast(I32), 0)
+        scale_table = reuse.tile([P, T], U8, name="scale_table", align_bytes=64, offset=3072)
+        nc.gpsimd.memset(scale_table[:].bitcast(I32), 0)
+        x_sc = sb([P, S], U8, "x_sc")
+        nc.vector.memset(x_sc[:].bitcast(I32), 0)
         ident = sb([P, P], F32, "ident")
         make_identity(nc, ident[:])
 
-        wide_rows = [sb([P, R], F32, "wide%d" % b) for b in range(2)]
+        wide_rows = [sb([P, R], F32, "wide0"), reuse.tile([P, R], F32, name="wide1", align_bytes=64, offset=4096)]
         nc.sync.dma_start(wide_rows[0][:], wide[0:P, :])
-        crosses = [load_list(cross1, "c1"), load_list(cross2, "c2"), load_list(cross3, "c3")]
+        users = load_list(offs, "users")
+        crosses = [load_list(cross1, "c1")]
+        nc.sync.dma_start(scale_table[32:96:4, :].bitcast(I32), x_scales[0].bitcast(I32))
+        crosses.append(load_list(cross2, "c2"))
+        crosses.append(load_list(cross3, "c3"))
         w1_raw = [sb([P, PACK, H // 2], F32, "w1_raw0"), reuse1.tile([P, PACK, H // 2], F32, name="w1_raw1", align_bytes=64, offset=0)]
         w1_view = w1.rearrange("(p j) c -> p j c", j=PACK)
         nc.sync.dma_start(w1_raw[0][:], w1_view[:, :, 0 : H // 2])
         nc.sync.dma_start(w1_raw[1][:], w1_view[:, :, H // 2 : H])
-        users = load_list(offs, "users")
-        for r in range(4):
-            nc.sync.dma_start(scale_table[r:P:32, :].bitcast(I32), x_scales[0, r:16:4, :].bitcast(I32))
         word_table = sb([P, T], I32, "word_table")
         nc.sync.dma_start(word_table[:], x_words[0].rearrange("p n t -> p (n t)").bitcast(I32))
+        sc_picked = sb([P, S], U8, "sc_picked")
+        nc.vector.tensor_copy(sc_picked[:], scale_table[:].indirect(users[:]))
+        for r in range(4):
+            nc.sync.dma_start(x_sc[r:P:32, :].bitcast(I32), sc_picked[32 + 4 * r : 96 : 16, :].bitcast(I32))
         w2_raw = reuse.tile([P, PACK, N], F32, name="w2_raw", align_bytes=64, offset=0)
         nc.sync.dma_start(w2_raw[:], w2.rearrange("(p j) c -> p j c", j=PACK))
         nc.sync.dma_start(wide_rows[1][:], wide[P : 2 * P, :])
@@ -85,8 +92,6 @@ def tile_picked_ywide_none_p_kernel(tc, x_words, x_scales, w1, w2, wide, offs, c
         turn_in(0)
         turn_in(1)
         turn_in(2)
-        x_sc = sb([P, S], U8, "x_sc")
-        nc.vector.tensor_copy(x_sc[:], scale_table[:].indirect(users[:]))
 
         w1_bf = sb([P, H * PACK], BF16, "w1_bf")
         for u in range(2):

@@ -52,10 +52,8 @@ def tile_picked_ywide_none_p_kernel(tc, x_words, x_scales, w1, w2, wide, offs, c
         nc.sync.dma_start(scale_table[32:96:4, :].bitcast(I32), x_scales[0].bitcast(I32))
         crosses.append(load_list(cross2, "c2"))
         crosses.append(load_list(cross3, "c3"))
-        w1_raw = [sb([P, PACK, H // 2], F32, "w1_raw0"), reuse1.tile([P, PACK, H // 2], F32, name="w1_raw1", align_bytes=64, offset=0)]
-        w1_view = w1.rearrange("(p j) c -> p j c", j=PACK)
-        nc.sync.dma_start(w1_raw[0][:], w1_view[:, :, 0 : H // 2])
-        nc.sync.dma_start(w1_raw[1][:], w1_view[:, :, H // 2 : H])
+        w1_raw = reuse1.tile([P, PACK, H], F32, name="w1_raw", align_bytes=64, offset=0)
+        nc.sync.dma_start(w1_raw[:], w1.rearrange("(p j) c -> p j c", j=PACK))
         word_table = sb([P, T], I32, "word_table")
         nc.sync.dma_start(word_table[:], x_words[0].rearrange("p n t -> p (n t)").bitcast(I32))
         sc_picked = sb([P, S], U8, "sc_picked")
@@ -94,12 +92,11 @@ def tile_picked_ywide_none_p_kernel(tc, x_words, x_scales, w1, w2, wide, offs, c
         turn_in(2)
 
         w1_bf = sb([P, H * PACK], BF16, "w1_bf")
-        for u in range(2):
-            nc.scalar.activation(
-                w1_bf[:].rearrange("p (t m j) -> p m j t", t=PACK, j=PACK)[:, u * P // 2 : (u + 1) * P // 2],
-                w1_raw[u][:].rearrange("p j (m t) -> p m j t", t=PACK),
-                COPY,
-            )
+        nc.scalar.activation(
+            w1_bf[:].rearrange("p (t m j) -> p m j t", t=PACK, j=PACK),
+            w1_raw[:].rearrange("p j (m t) -> p m j t", t=PACK),
+            COPY,
+        )
 
         def quantise(src, width, name):
             codes = sb([P, width], U32, name + "_codes")

@@ -17,9 +17,10 @@ RELU = mybir.ActivationFunctionType.Relu
 K, T, S, H, N, R = 512, 2048, 512, 512, 256, 1024
 P = 128
 PACK = 4
-CHUNK = 128
-FLOPS = 2 * K * H * S + 2 * H * N * S
+BLOCKS = K // 32
+SCALE_ROW0 = P - BLOCKS
 HALF = S // 2
+FLOPS = 2 * K * H * S + 2 * H * N * S
 
 
 def tile_picked_ywide_none_p_kernel(tc, x_words, x_scales, w1, w2, wide, offs, cross1, cross2, cross3, out):
@@ -27,7 +28,6 @@ def tile_picked_ywide_none_p_kernel(tc, x_words, x_scales, w1, w2, wide, offs, c
     with ExitStack() as ctx:
         keep = ctx.enter_context(tc.tile_pool(name="keep", bufs=1))
         reuse = ctx.enter_context(tc.tile_pool(name="reuse", bufs=1))
-        reuse1 = ctx.enter_context(tc.tile_pool(name="reuse1", bufs=1))
         psum = ctx.enter_context(tc.psum_pool(name="psum", bufs=1))
 
         def sb(shape, dtype, name):
@@ -39,64 +39,61 @@ def tile_picked_ywide_none_p_kernel(tc, x_words, x_scales, w1, w2, wide, offs, c
             return t
 
         scale_table = reuse.tile([P, T], U8, name="scale_table", align_bytes=64, offset=3072)
-        nc.gpsimd.memset(scale_table[:].bitcast(I32), 0)
+        nc.sync.dma_start(scale_table[SCALE_ROW0:P, :].bitcast(I32), x_scales[0].bitcast(I32))
+        users = load_list(offs, "users")
+        nc.vector.memset(scale_table[0:SCALE_ROW0, :].bitcast(I32), 0)
         x_sc = sb([P, S], U8, "x_sc")
-        nc.vector.memset(x_sc[:].bitcast(I32), 0)
+        nc.gpsimd.memset(x_sc[:].bitcast(I32), 0)
         ident = sb([P, P], F32, "ident")
         make_identity(nc, ident[:])
 
         wide_rows = [sb([P, R], F32, "wide0"), reuse.tile([P, R], F32, name="wide1", align_bytes=64, offset=4096)]
         nc.sync.dma_start(wide_rows[0][:], wide[0:P, :])
-        users = load_list(offs, "users")
-        crosses = [load_list(cross1, "c1")]
-        nc.sync.dma_start(scale_table[32:96:4, :].bitcast(I32), x_scales[0].bitcast(I32))
-        crosses.append(load_list(cross2, "c2"))
-        crosses.append(load_list(cross3, "c3"))
-        w1_raw = reuse1.tile([P, PACK, H], F32, name="w1_raw", align_bytes=64, offset=0)
-        nc.sync.dma_start(w1_raw[:], w1.rearrange("(p j) c -> p j c", j=PACK))
+        crosses = [load_list(cross1, "c1"), load_list(cross2, "c2"), load_list(cross3, "c3")]
+        w1_raw = [sb([P, PACK, H // 2], F32, "w1_raw0"), reuse.tile([P, PACK, H // 2], F32, name="w1_raw1", align_bytes=64, offset=8192)]
+        for u in range(2):
+            nc.sync.dma_start(w1_raw[u][:], w1.rearrange("(p j) c -> p j c", j=PACK)[:, :, u * H // 2 : (u + 1) * H // 2])
         word_table = sb([P, T], I32, "word_table")
         nc.sync.dma_start(word_table[:], x_words[0].rearrange("p n t -> p (n t)").bitcast(I32))
         sc_picked = sb([P, S], U8, "sc_picked")
         nc.vector.tensor_copy(sc_picked[:], scale_table[:].indirect(users[:]))
         for r in range(4):
-            nc.sync.dma_start(x_sc[r:P:32, :].bitcast(I32), sc_picked[32 + 4 * r : 96 : 16, :].bitcast(I32))
+            nc.sync.dma_start(x_sc[r:P:32, :].bitcast(I32), sc_picked[SCALE_ROW0 + r : P : 4, :].bitcast(I32))
         w2_raw = reuse.tile([P, PACK, N], F32, name="w2_raw", align_bytes=64, offset=0)
         nc.sync.dma_start(w2_raw[:], w2.rearrange("(p j) c -> p j c", j=PACK))
         nc.sync.dma_start(wide_rows[1][:], wide[P : 2 * P, :])
 
-        second = [sb([P, HALF], F32, "second%d" % u) for u in range(2)]
-        for u in range(2):
-            nc.gpsimd.memset(second[u][:, 0:1], 0.0)
-        zeros = [0.0, second[0][:, 0:1], 0.0, second[1][:, 0:1]]
-
         def picked(b, i, first, count):
             return wide_rows[b][:].indirect(crosses[i][:, first // 16 : (first + count) // 16])
 
-        turned = psum.tile([P, S // P, P], F32, name="turned")
+        def turn(dst, sources):
+            pieces = dst.shape[1]
+            for k, src in enumerate(sources):
+                for c in range(pieces):
+                    nc.tensor.matmul(
+                        dst[:, c, :], src(c), ident[:],
+                        start=(k == 0 and c == 0), stop=(k == len(sources) - 1 and c == pieces - 1), is_transpose=True,
+                    )
 
-        def turn_in(i):
-            g = sb([P, S], F32, "g%d" % i)
-            nc.vector.tensor_copy(g[:], picked(0, i, 0, S))
-            for c in range(S // P):
-                nc.tensor.matmul(
-                    turned[:, c, :],
-                    g[:, c * P : (c + 1) * P],
-                    ident[:],
-                    start=(i == 0 and c == 0),
-                    stop=(i == 2 and c == S // P - 1),
-                    is_transpose=True,
-                )
+        def columns(t, first=0):
+            return lambda c: t[:, first + c * P : first + (c + 1) * P]
 
-        turn_in(0)
-        turn_in(1)
-        turn_in(2)
+        looked0 = [sb([P, S], F32, "looked0_%d" % i) for i in range(3)]
+        for i in range(3):
+            nc.vector.tensor_copy(looked0[i][:], picked(0, i, 0, S))
+        turned0 = psum.tile([P, S // P, P], F32, name="turned0")
+        turn(turned0, [columns(t) for t in looked0])
 
         w1_bf = sb([P, H * PACK], BF16, "w1_bf")
-        nc.scalar.activation(
-            w1_bf[:].rearrange("p (t m j) -> p m j t", t=PACK, j=PACK),
-            w1_raw[:].rearrange("p j (m t) -> p m j t", t=PACK),
-            COPY,
-        )
+        w1_dst = w1_bf[:].rearrange("p (t m j) -> p m j t", t=PACK, j=PACK)
+        for u in range(2):
+            nc.scalar.activation(
+                w1_dst[:, u * P // 2 : (u + 1) * P // 2],
+                w1_raw[u][:].rearrange("p j (m t) -> p m j t", t=PACK),
+                COPY,
+            )
+        turned0_sb = reuse.tile([P, S], F32, name="turned0_sb", align_bytes=64, offset=8192)
+        nc.scalar.copy(turned0_sb[:], turned0[:].rearrange("p c n -> p (c n)"))
 
         def quantise(src, width, name):
             codes = sb([P, width], U32, name + "_codes")
@@ -117,76 +114,84 @@ def tile_picked_ywide_none_p_kernel(tc, x_words, x_scales, w1, w2, wide, offs, c
 
         w1_mx = quantise(w1_bf, H, "w1")
 
-        turned_sb = reuse1.tile([P, S], F32, name="turned_sb", align_bytes=64, offset=5 * S)
-        nc.scalar.copy(turned_sb[:], turned[:].rearrange("p c n -> p (c n)"))
-
-        x_codes = reuse1.tile([P, S], U32, name="x_codes", align_bytes=64, offset=0)
+        x_codes = reuse.tile([P, S], U32, name="x_codes", align_bytes=64, offset=10240)
         for u in range(2):
             nc.vector.tensor_copy(
                 x_codes[:, u * HALF : (u + 1) * HALF],
                 word_table[:].bitcast(U32).indirect(users[:, u * HALF // 16 : (u + 1) * HALF // 16]),
             )
 
-        w2_bf = sb([P, N * PACK], BF16, "w2_bf")
-        w2_dst = w2_bf[:].rearrange("p (c i j) -> p c j i", i=4, j=PACK)
-        w2_src = w2_raw[:].rearrange("p j (c i) -> p c j i", i=4)
-        nc.scalar.activation(w2_dst[:, 0:32], w2_src[:, 0:32], COPY)
-        nc.vector.tensor_copy(w2_dst[:, 32:64], w2_src[:, 32:64])
+        w2_bf = [sb([P, P * PACK], BF16, "w2_bf%d" % b) for b in range(2)]
+        for b in range(2):
+            nc.vector.tensor_copy(
+                w2_bf[b][:].rearrange("p (c i j) -> p c j i", i=4, j=PACK),
+                w2_raw[:, :, b * P : (b + 1) * P].rearrange("p j (c i) -> p c j i", i=4),
+            )
+        w2_codes = sb([P, N], U32, "w2_codes")
+        w2_sc = sb([P, N], U8, "w2_sc")
+        for b in range(2):
+            nc.vector.quantize_mx(out=w2_codes[:, b * P : (b + 1) * P].bitcast(FP8X4), scales=w2_sc[:, b * P : (b + 1) * P], in_=w2_bf[b][:])
+        w2_mx = (w2_codes, w2_sc)
 
-        h_bf = [
-            reuse.tile([P, HALF * PACK], BF16, name="h_bf0", align_bytes=64, offset=0),
-            reuse.tile([P, HALF * PACK], BF16, name="h_bf1", tag="h_bf1", align_bytes=64, offset=2 * HALF * PACK),
-        ]
-        for c in range(S // CHUNK):
+        h_bf = [sb([P, HALF * PACK], BF16, "h_bf%d" % u) for u in range(2)]
+        looked1 = [sb([P, HALF], F32, "looked1_%d" % i) for i in range(2)]
+        nc.gpsimd.memset(looked1[1][:, 0:1], 0.0)
+        for c in range(S // P):
             u, e = divmod(c, 2)
-            bank = psum.tile([P, PACK, CHUNK], F32, name="hbank%d" % c, tag="bank%d" % c)
+            bank = psum.tile([P, PACK, P], F32, name="hbank%d" % c, tag="bank%d" % c)
             for t in range(PACK):
-                product(bank[:, t, :], w1_mx, slice(t * P, (t + 1) * P), (x_codes, x_sc), slice(c * CHUNK, (c + 1) * CHUNK))
+                product(bank[:, t, :], w1_mx, slice(t * P, (t + 1) * P), (x_codes, x_sc), slice(c * P, (c + 1) * P))
             nc.scalar.activation(
-                h_bf[u][:, e * CHUNK * PACK : (e + 1) * CHUNK * PACK].rearrange("p (n t) -> p n t", t=PACK),
+                h_bf[u][:, e * P * PACK : (e + 1) * P * PACK].rearrange("p (n t) -> p n t", t=PACK),
                 bank[:].rearrange("p t n -> p n t"),
                 RELU,
-                bias=zeros[c],
+                bias=looked1[1][:, 0:1] if c == 1 else 0.0,
             )
 
-        w2_mx = quantise(w2_bf, N, "w2")
-        first = sb([P, S], F32, "first")
-        nc.vector.tensor_copy(first[:], picked(1, 0, 0, S))
+        h0_mx = quantise(h_bf[0], HALF, "h0")
+        y_lo = psum.tile([P, S], F32, name="y_lo")
+        product(y_lo[:, 0:HALF], w2_mx, slice(P, 2 * P), h0_mx, slice(0, HALF))
+        for e in range(2):
+            product(y_lo[:, HALF + e * P : HALF + (e + 1) * P], h0_mx, slice(e * P, (e + 1) * P), w2_mx, slice(0, P))
+        y_lo_sb = sb([P, S], F32, "y_lo_sb")
+        nc.scalar.copy(y_lo_sb[:], y_lo[:])
 
+        for i in range(2):
+            nc.vector.tensor_copy(looked1[i][:], picked(1, i, HALF, HALF))
+        turned1 = psum.tile([P, 2, P], F32, name="turned1", tag="bank3")
+        turn(turned1, [columns(t) for t in looked1])
+        turned1_sb = sb([P, HALF], F32, "turned1_sb")
+        nc.scalar.copy(turned1_sb[:], turned1[:].rearrange("p c n -> p (c n)"))
 
-        h_mx = []
-        y1 = []
-        y0_sb = []
-        for u in range(2):
-            h_mx.append(quantise(h_bf[u], HALF, "h%d" % u))
-            yt = psum.tile([P, 2, P], F32, name="y0_%d" % u)
-            for e in range(2):
-                product(yt[:, e, :], h_mx[u], slice(e * P, (e + 1) * P), w2_mx, slice(0, P))
-            yb = psum.tile([P, HALF], F32, name="y1_%d" % u, tag="bank%d" % (2 * u))
-            product(yb[:], w2_mx, slice(P, 2 * P), h_mx[u], slice(0, HALF))
-            y1.append(yb)
-            ys = sb([P, HALF], F32, "y0_sb%d" % u)
-            nc.scalar.copy(ys[:], yt[:].rearrange("p e n -> p (e n)"))
-            y0_sb.append(ys)
-            nc.vector.tensor_tensor(second[u][:], picked(1, 1, u * HALF, HALF), first[:, u * HALF : (u + 1) * HALF], ADD)
+        h1_mx = quantise(h_bf[1], HALF, "h1")
+        y_hi = psum.tile([P, 2, N], F32, name="y_hi")
+        for e in range(2):
+            product(y_hi[:, e, :], h1_mx, slice(e * P, (e + 1) * P), w2_mx, slice(0, N))
+        y_hi_sb = sb([P, 2, N], F32, "y_hi_sb")
+        nc.scalar.copy(y_hi_sb[:], y_hi[:])
 
-        third = [reuse.tile([P, HALF], F32, name="third0", tag="h_bf1", align_bytes=64, offset=2 * HALF * PACK), sb([P, HALF], F32, "third1")]
-        for u in range(2):
-            nc.vector.tensor_tensor(third[u][:], y1[u][:], second[u][:], ADD)
-        for lo, hi in ((0, HALF), (HALF, HALF + P), (HALF + P, S)):
-            res = sb([P, hi - lo], F32, "res1_%d" % lo)
-            u = lo // HALF
-            nc.vector.tensor_tensor(res[:], picked(1, 2, lo, hi - lo), third[u][:, lo - u * HALF : hi - u * HALF], ADD)
-            nc.sync.dma_start(out[P : 2 * P, lo:hi], res[:])
-
-        for u in range(2):
-            back = psum.tile([P, 2, P], F32, name="back%d" % u, tag="bank%d" % (2 * u + 1))
-            for k, src in enumerate((turned_sb[:, u * HALF : (u + 1) * HALF], y0_sb[u][:])):
-                for e in range(2):
-                    nc.tensor.matmul(
-                        back[:, e, :], src[:, e * P : (e + 1) * P], ident[:],
-                        start=(k == 0 and e == 0), stop=(k == 1 and e == 1), is_transpose=True,
-                    )
-            res = sb([P, HALF], F32, "res0_%d" % u)
+        def merge(name, tag, sources):
+            back = psum.tile([P, 2, P], F32, name=name + "_ps", tag=tag)
+            turn(back, sources)
+            res = sb([P, HALF], F32, name)
             nc.scalar.copy(res[:], back[:].rearrange("p e n -> p (e n)"))
-            nc.scalar.dma_start(out[0:P, u * HALF : (u + 1) * HALF], res[:])
+            return res
+
+        res = merge("res0_lo", "bank0", [columns(turned0_sb), columns(y_lo_sb, HALF)])
+        nc.scalar.dma_start(out[0:P, 0:HALF], res[:])
+
+        partial = y_lo_sb
+        for i in range(3):
+            nxt = sb([P, HALF], F32, "chain%d" % i)
+            for e in range(2):
+                nc.vector.tensor_tensor(nxt[:, e * P : (e + 1) * P], picked(1, i, e * P, P), partial[:, e * P : (e + 1) * P], ADD)
+            partial = nxt
+        nc.sync.dma_start(out[P : 2 * P, 0:HALF], partial[:])
+
+        merged = merge("merged1", "bank1", [columns(turned1_sb), lambda c: y_hi_sb[:, c, P : 2 * P]])
+        res = merge("res0_hi", "bank2", [columns(turned0_sb, HALF), lambda c: y_hi_sb[:, c, 0:P]])
+        nc.scalar.dma_start(out[0:P, HALF:S], res[:])
+        for e in range(2):
+            last = sb([P, P], F32, "last%d" % e)
+            nc.vector.tensor_tensor(last[:], picked(1, 2, HALF + e * P, P), merged[:, e * P : (e + 1) * P], ADD)
+            nc.sync.dma_start(out[P : 2 * P, HALF + e * P : HALF + (e + 1) * P], last[:])

@@ -39,7 +39,7 @@ def tile_picked_ywide_none_p_kernel(tc, x_words, x_scales, w1, w2, wide, offs, c
             return t
 
         scale_table = reuse.tile([P, T], U8, name="scale_table", align_bytes=64, offset=3072)
-        nc.sync.dma_start(scale_table[SCALE_ROW0:P, :].bitcast(I32), x_scales[0].bitcast(I32))
+        nc.scalar.dma_start(scale_table[SCALE_ROW0:P, :].bitcast(I32), x_scales[0].bitcast(I32))
         users = load_list(offs, "users")
         nc.vector.memset(scale_table[0:SCALE_ROW0, :].bitcast(I32), 0)
         x_sc = sb([P, S], U8, "x_sc")
@@ -134,8 +134,10 @@ def tile_picked_ywide_none_p_kernel(tc, x_words, x_scales, w1, w2, wide, offs, c
         w2_mx = (w2_codes, w2_sc)
 
         h_bf = [sb([P, HALF * PACK], BF16, "h_bf%d" % u) for u in range(2)]
-        looked1 = [sb([P, HALF], F32, "looked1_%d" % i) for i in range(2)]
-        nc.gpsimd.memset(looked1[1][:, 0:1], 0.0)
+        early = [sb([P, HALF], F32, "early%d" % i) for i in range(3)]
+        for i in (1, 2):
+            nc.gpsimd.memset(early[i][:, 0:1], 0.0)
+        zeros = [0.0, early[1][:, 0:1], 0.0, early[2][:, 0:1]]
         for c in range(S // P):
             u, e = divmod(c, 2)
             bank = psum.tile([P, PACK, P], F32, name="hbank%d" % c, tag="bank%d" % c)
@@ -145,53 +147,47 @@ def tile_picked_ywide_none_p_kernel(tc, x_words, x_scales, w1, w2, wide, offs, c
                 h_bf[u][:, e * P * PACK : (e + 1) * P * PACK].rearrange("p (n t) -> p n t", t=PACK),
                 bank[:].rearrange("p t n -> p n t"),
                 RELU,
-                bias=looked1[1][:, 0:1] if c == 1 else 0.0,
+                bias=zeros[c],
             )
 
-        h0_mx = quantise(h_bf[0], HALF, "h0")
-        y_lo = psum.tile([P, S], F32, name="y_lo")
-        product(y_lo[:, 0:HALF], w2_mx, slice(P, 2 * P), h0_mx, slice(0, HALF))
-        for e in range(2):
-            product(y_lo[:, HALF + e * P : HALF + (e + 1) * P], h0_mx, slice(e * P, (e + 1) * P), w2_mx, slice(0, P))
-        y_lo_sb = sb([P, S], F32, "y_lo_sb")
-        nc.scalar.copy(y_lo_sb[:], y_lo[:])
-
-        for i in range(2):
-            nc.vector.tensor_copy(looked1[i][:], picked(1, i, HALF, HALF))
-        turned1 = psum.tile([P, 2, P], F32, name="turned1", tag="bank3")
-        turn(turned1, [columns(t) for t in looked1])
-        turned1_sb = sb([P, HALF], F32, "turned1_sb")
-        nc.scalar.copy(turned1_sb[:], turned1[:].rearrange("p c n -> p (c n)"))
-
-        h1_mx = quantise(h_bf[1], HALF, "h1")
-        y_hi = psum.tile([P, 2, N], F32, name="y_hi")
-        for e in range(2):
-            product(y_hi[:, e, :], h1_mx, slice(e * P, (e + 1) * P), w2_mx, slice(0, N))
-        y_hi_sb = sb([P, 2, N], F32, "y_hi_sb")
-        nc.scalar.copy(y_hi_sb[:], y_hi[:])
-
-        def merge(name, tag, sources):
-            back = psum.tile([P, 2, P], F32, name=name + "_ps", tag=tag)
-            turn(back, sources)
-            res = sb([P, HALF], F32, name)
-            nc.scalar.copy(res[:], back[:].rearrange("p e n -> p (e n)"))
-            return res
-
-        res = merge("res0_lo", "bank0", [columns(turned0_sb), columns(y_lo_sb, HALF)])
-        nc.scalar.dma_start(out[0:P, 0:HALF], res[:])
-
-        partial = y_lo_sb
-        for i in range(3):
-            nxt = sb([P, HALF], F32, "chain%d" % i)
+        def products(u):
+            h_mx = quantise(h_bf[u], HALF, "h%d" % u)
+            y0t = psum.tile([P, 2, P], F32, name="y0t_%d" % u)
+            y1 = psum.tile([P, HALF], F32, name="y1_%d" % u, tag="bank%d" % (2 * u))
+            if u == 0:
+                product(y1[:], w2_mx, slice(P, 2 * P), h_mx, slice(0, HALF))
             for e in range(2):
-                nc.vector.tensor_tensor(nxt[:, e * P : (e + 1) * P], picked(1, i, e * P, P), partial[:, e * P : (e + 1) * P], ADD)
-            partial = nxt
-        nc.sync.dma_start(out[P : 2 * P, 0:HALF], partial[:])
+                product(y0t[:, e, :], h_mx, slice(e * P, (e + 1) * P), w2_mx, slice(0, P))
+            if u == 1:
+                product(y1[:], w2_mx, slice(P, 2 * P), h_mx, slice(0, HALF))
+            return y0t, y1
 
-        merged = merge("merged1", "bank1", [columns(turned1_sb), lambda c: y_hi_sb[:, c, P : 2 * P]])
-        res = merge("res0_hi", "bank2", [columns(turned0_sb, HALF), lambda c: y_hi_sb[:, c, 0:P]])
-        nc.scalar.dma_start(out[0:P, HALF:S], res[:])
+        def finish_block0(u, y0t):
+            y0t_sb = sb([P, HALF], F32, "y0t_sb%d" % u)
+            nc.scalar.copy(y0t_sb[:], y0t[:].rearrange("p e n -> p (e n)"))
+            back = psum.tile([P, 2, P], F32, name="back%d" % u, tag="bank%d" % (2 * u + 1))
+            turn(back, [columns(turned0_sb, u * HALF), columns(y0t_sb)])
+            res = sb([P, HALF], F32, "res0_%d" % u)
+            nc.scalar.copy(res[:], back[:].rearrange("p e n -> p (e n)"))
+            nc.scalar.dma_start(out[0:P, u * HALF : (u + 1) * HALF], res[:])
+
+        nc.vector.tensor_copy(early[0][:], picked(1, 0, HALF, HALF))
+        y0t_lo, y1_lo = products(0)
+        nc.vector.tensor_tensor(early[1][:], picked(1, 1, HALF, HALF), early[0][:], ADD)
+        y0t_hi, y1_hi = products(1)
+        y1_lo_sb = sb([P, HALF], F32, "y1_lo_sb")
+        nc.scalar.copy(y1_lo_sb[:], y1_lo[:])
+        nc.vector.tensor_tensor(early[2][:], picked(1, 2, HALF, HALF), early[1][:], ADD)
+        late = [sb([P, HALF], F32, "late%d" % i) for i in range(2)]
+        nc.vector.tensor_tensor(late[0][:], picked(1, 0, 0, HALF), y1_lo_sb[:], ADD)
+        res_hi = sb([P, HALF], F32, "res1_hi")
+        nc.vector.tensor_tensor(res_hi[:], y1_hi[:], early[2][:], ADD)
+        nc.sync.dma_start(out[P : 2 * P, HALF:S], res_hi[:])
+        for e in range(2):
+            nc.vector.tensor_tensor(late[1][:, e * P : (e + 1) * P], picked(1, 1, e * P, P), late[0][:, e * P : (e + 1) * P], ADD)
         for e in range(2):
             last = sb([P, P], F32, "last%d" % e)
-            nc.vector.tensor_tensor(last[:], picked(1, 2, HALF + e * P, P), merged[:, e * P : (e + 1) * P], ADD)
-            nc.sync.dma_start(out[P : 2 * P, HALF + e * P : HALF + (e + 1) * P], last[:])
+            nc.vector.tensor_tensor(last[:], picked(1, 2, e * P, P), late[1][:, e * P : (e + 1) * P], ADD)
+            nc.sync.dma_start(out[P : 2 * P, e * P : (e + 1) * P], last[:])
+        finish_block0(0, y0t_lo)
+        finish_block0(1, y0t_hi)

@@ -121,23 +121,18 @@ def tile_picked_ywide_none_p_kernel(tc, x_words, x_scales, w1, w2, wide, offs, c
                 word_table[:].bitcast(U32).indirect(users[:, u * HALF // 16 : (u + 1) * HALF // 16]),
             )
 
-        w2_bf = [sb([P, P * PACK], BF16, "w2_bf%d" % b) for b in range(2)]
-        for b in range(2):
-            nc.vector.tensor_copy(
-                w2_bf[b][:].rearrange("p (c i j) -> p c j i", i=4, j=PACK),
-                w2_raw[:, :, b * P : (b + 1) * P].rearrange("p j (c i) -> p c j i", i=4),
-            )
-        w2_codes = sb([P, N], U32, "w2_codes")
-        w2_sc = sb([P, N], U8, "w2_sc")
-        for b in range(2):
-            nc.vector.quantize_mx(out=w2_codes[:, b * P : (b + 1) * P].bitcast(FP8X4), scales=w2_sc[:, b * P : (b + 1) * P], in_=w2_bf[b][:])
-        w2_mx = (w2_codes, w2_sc)
+        w2_bf = sb([P, N * PACK], BF16, "w2_bf")
+        w2_dst = w2_bf[:].rearrange("p (c i j) -> p c j i", i=4, j=PACK)
+        w2_src = w2_raw[:].rearrange("p j (c i) -> p c j i", i=4)
+        nc.scalar.activation(w2_dst[:, 0:32], w2_src[:, 0:32], COPY)
+        nc.vector.tensor_copy(w2_dst[:, 32:64], w2_src[:, 32:64])
+        w2_mx = quantise(w2_bf, N, "w2")
 
-        h_bf = [sb([P, HALF * PACK], BF16, "h_bf%d" % u) for u in range(2)]
-        early = [sb([P, HALF], F32, "early%d" % i) for i in range(3)]
-        for i in (1, 2):
-            nc.gpsimd.memset(early[i][:, 0:1], 0.0)
-        zeros = [0.0, early[1][:, 0:1], 0.0, early[2][:, 0:1]]
+        h_bf = [reuse.tile([P, HALF * PACK], BF16, name="h_bf%d" % u, align_bytes=64, offset=u * 2048) for u in range(2)]
+        early = [sb([P, S], F32, "early%d" % i) for i in range(2)]
+        zeros = [0.0, early[1][:, 0:1], 0.0, early[1][:, HALF : HALF + 1]]
+        for z in zeros[1::2]:
+            nc.gpsimd.memset(z, 0.0)
         for c in range(S // P):
             u, e = divmod(c, 2)
             bank = psum.tile([P, PACK, P], F32, name="hbank%d" % c, tag="bank%d" % c)
@@ -154,12 +149,9 @@ def tile_picked_ywide_none_p_kernel(tc, x_words, x_scales, w1, w2, wide, offs, c
             h_mx = quantise(h_bf[u], HALF, "h%d" % u)
             y0t = psum.tile([P, 2, P], F32, name="y0t_%d" % u)
             y1 = psum.tile([P, HALF], F32, name="y1_%d" % u, tag="bank%d" % (2 * u))
-            if u == 0:
-                product(y1[:], w2_mx, slice(P, 2 * P), h_mx, slice(0, HALF))
             for e in range(2):
                 product(y0t[:, e, :], h_mx, slice(e * P, (e + 1) * P), w2_mx, slice(0, P))
-            if u == 1:
-                product(y1[:], w2_mx, slice(P, 2 * P), h_mx, slice(0, HALF))
+            product(y1[:], w2_mx, slice(P, 2 * P), h_mx, slice(0, HALF))
             return y0t, y1
 
         def finish_block0(u, y0t):
@@ -171,23 +163,19 @@ def tile_picked_ywide_none_p_kernel(tc, x_words, x_scales, w1, w2, wide, offs, c
             nc.scalar.copy(res[:], back[:].rearrange("p e n -> p (e n)"))
             nc.scalar.dma_start(out[0:P, u * HALF : (u + 1) * HALF], res[:])
 
-        nc.vector.tensor_copy(early[0][:], picked(1, 0, HALF, HALF))
+        nc.vector.tensor_copy(early[0][:], picked(1, 0, 0, S))
         y0t_lo, y1_lo = products(0)
-        nc.vector.tensor_tensor(early[1][:], picked(1, 1, HALF, HALF), early[0][:], ADD)
+        nc.vector.tensor_tensor(early[1][:, 0:HALF], picked(1, 1, 0, HALF), early[0][:, 0:HALF], ADD)
         y0t_hi, y1_hi = products(1)
-        y1_lo_sb = sb([P, HALF], F32, "y1_lo_sb")
-        nc.scalar.copy(y1_lo_sb[:], y1_lo[:])
-        nc.vector.tensor_tensor(early[2][:], picked(1, 2, HALF, HALF), early[1][:], ADD)
-        late = [sb([P, HALF], F32, "late%d" % i) for i in range(2)]
-        nc.vector.tensor_tensor(late[0][:], picked(1, 0, 0, HALF), y1_lo_sb[:], ADD)
-        res_hi = sb([P, HALF], F32, "res1_hi")
-        nc.vector.tensor_tensor(res_hi[:], y1_hi[:], early[2][:], ADD)
-        nc.sync.dma_start(out[P : 2 * P, HALF:S], res_hi[:])
-        for e in range(2):
-            nc.vector.tensor_tensor(late[1][:, e * P : (e + 1) * P], picked(1, 1, e * P, P), late[0][:, e * P : (e + 1) * P], ADD)
-        for e in range(2):
-            last = sb([P, P], F32, "last%d" % e)
-            nc.vector.tensor_tensor(last[:], picked(1, 2, e * P, P), late[1][:, e * P : (e + 1) * P], ADD)
-            nc.sync.dma_start(out[P : 2 * P, e * P : (e + 1) * P], last[:])
+        nc.vector.tensor_tensor(early[1][:, HALF:S], picked(1, 1, HALF, HALF), early[0][:, HALF:S], ADD)
+        summed = [reuse.tile([P, HALF], F32, name="summed0", align_bytes=64, offset=2048), sb([P, HALF], F32, "summed1")]
+        for u in range(2):
+            cols = slice(u * HALF, (u + 1) * HALF)
+            nc.vector.tensor_tensor(summed[u][:], picked(1, 2, u * HALF, HALF), early[1][:, cols], ADD)
+        for u, y1 in enumerate((y1_lo, y1_hi)):
+            cols = slice(u * HALF, (u + 1) * HALF)
+            res = sb([P, HALF], F32, "res1_%d" % u)
+            nc.vector.tensor_tensor(res[:], y1[:], summed[u][:], ADD)
+            nc.sync.dma_start(out[P : 2 * P, cols], res[:])
         finish_block0(0, y0t_lo)
         finish_block0(1, y0t_hi)

@@ -1,7 +1,6 @@
 from contextlib import ExitStack
 
 import concourse.mybir as mybir
-from concourse.masks import make_identity
 
 F32 = mybir.dt.float32
 BF16 = mybir.dt.bfloat16
@@ -33,67 +32,13 @@ def tile_picked_ywide_none_p_kernel(tc, x_words, x_scales, w1, w2, wide, offs, c
         def sb(shape, dtype, name):
             return keep.tile(shape, dtype, name=name, align_bytes=64)
 
+        def placed(shape, dtype, name, offset):
+            return reuse.tile(shape, dtype, name=name, align_bytes=64, offset=offset)
+
         def load_list(src, name):
             t = keep.tile([P, S // 16], U16, name=name)
             nc.sync.dma_start(t[:], src)
             return t
-
-        scale_table = reuse.tile([P, T], U8, name="scale_table", align_bytes=64, offset=3072)
-        nc.scalar.dma_start(scale_table[SCALE_ROW0:P, :].bitcast(I32), x_scales[0].bitcast(I32))
-        users = load_list(offs, "users")
-        nc.vector.memset(scale_table[0:SCALE_ROW0, :].bitcast(I32), 0)
-        x_sc = sb([P, S], U8, "x_sc")
-        nc.gpsimd.memset(x_sc[:].bitcast(I32), 0)
-        ident = sb([P, P], F32, "ident")
-        make_identity(nc, ident[:])
-
-        wide_rows = [sb([P, R], F32, "wide0"), reuse.tile([P, R], F32, name="wide1", align_bytes=64, offset=4096)]
-        nc.sync.dma_start(wide_rows[0][:], wide[0:P, :])
-        crosses = [load_list(cross1, "c1"), load_list(cross2, "c2"), load_list(cross3, "c3")]
-        w1_raw = [sb([P, PACK, H // 2], F32, "w1_raw0"), reuse.tile([P, PACK, H // 2], F32, name="w1_raw1", align_bytes=64, offset=8192)]
-        for u in range(2):
-            nc.sync.dma_start(w1_raw[u][:], w1.rearrange("(p j) c -> p j c", j=PACK)[:, :, u * H // 2 : (u + 1) * H // 2])
-        word_table = sb([P, T], I32, "word_table")
-        nc.sync.dma_start(word_table[:], x_words[0].rearrange("p n t -> p (n t)").bitcast(I32))
-        sc_picked = sb([P, S], U8, "sc_picked")
-        nc.vector.tensor_copy(sc_picked[:], scale_table[:].indirect(users[:]))
-        for r in range(4):
-            nc.sync.dma_start(x_sc[r:P:32, :].bitcast(I32), sc_picked[SCALE_ROW0 + r : P : 4, :].bitcast(I32))
-        w2_raw = reuse.tile([P, PACK, N], F32, name="w2_raw", align_bytes=64, offset=0)
-        nc.sync.dma_start(w2_raw[:], w2.rearrange("(p j) c -> p j c", j=PACK))
-        nc.sync.dma_start(wide_rows[1][:], wide[P : 2 * P, :])
-
-        def picked(b, i, first, count):
-            return wide_rows[b][:].indirect(crosses[i][:, first // 16 : (first + count) // 16])
-
-        def turn(dst, sources):
-            pieces = dst.shape[1]
-            for k, src in enumerate(sources):
-                for c in range(pieces):
-                    nc.tensor.matmul(
-                        dst[:, c, :], src(c), ident[:],
-                        start=(k == 0 and c == 0), stop=(k == len(sources) - 1 and c == pieces - 1), is_transpose=True,
-                    )
-
-        def columns(t, first=0):
-            return lambda c: t[:, first + c * P : first + (c + 1) * P]
-
-        looked0 = [sb([P, S], F32, "looked0_%d" % i) for i in range(3)]
-        for i in range(3):
-            nc.vector.tensor_copy(looked0[i][:], picked(0, i, 0, S))
-        turned0 = psum.tile([P, S // P, P], F32, name="turned0")
-        turn(turned0, [columns(t) for t in looked0])
-
-        w1_bf = sb([P, H * PACK], BF16, "w1_bf")
-        w1_dst = w1_bf[:].rearrange("p (t m j) -> p m j t", t=PACK, j=PACK)
-        for u in range(2):
-            nc.scalar.activation(
-                w1_dst[:, u * P // 2 : (u + 1) * P // 2],
-                w1_raw[u][:].rearrange("p j (m t) -> p m j t", t=PACK),
-                COPY,
-            )
-        turned0_sb = reuse.tile([P, S], F32, name="turned0_sb", align_bytes=64, offset=8192)
-        nc.scalar.copy(turned0_sb[:], turned0[:].rearrange("p c n -> p (c n)"))
 
         def quantise(src, width, name):
             codes = sb([P, width], U32, name + "_codes")
@@ -112,70 +57,89 @@ def tile_picked_ywide_none_p_kernel(tc, x_words, x_scales, w1, w2, wide, offs, c
                 stop=True,
             )
 
-        w1_mx = quantise(w1_bf, H, "w1")
+        scale_table = placed([P, T], U8, "scale_table", 3072)
+        nc.scalar.dma_start(scale_table[SCALE_ROW0:P, :].bitcast(I32), x_scales[0].bitcast(I32))
+        users = load_list(offs, "users")
+        nc.vector.memset(scale_table[0:SCALE_ROW0, :].bitcast(I32), 0)
+        zero_seed = sb([P, 1], F32, "zero_seed")
+        nc.gpsimd.memset(zero_seed[:], 0.0)
+        relu_bias = sb([P, 1], F32, "relu_bias")
+        nc.scalar.activation(relu_bias[:], zero_seed[:], COPY)
+        x_sc = sb([P, S], U8, "x_sc")
+        nc.gpsimd.memset(x_sc[:].bitcast(I32), 0)
 
-        x_codes = reuse.tile([P, S], U32, name="x_codes", align_bytes=64, offset=10240)
+        wide_rows = [sb([P, R], F32, "wide%d" % b) for b in range(2)]
+        nc.sync.dma_start(wide_rows[0][:], wide[0:P, :])
+        crosses = [load_list(cross1, "c1"), load_list(cross2, "c2")]
+        nc.sync.dma_start(wide_rows[1][:], wide[P : 2 * P, :])
+        w1_raw = [sb([P, PACK, H // 2], F32, "w1_raw%d" % u) for u in range(2)]
         for u in range(2):
+            nc.sync.dma_start(w1_raw[u][:], w1.rearrange("(p j) c -> p j c", j=PACK)[:, :, u * H // 2 : (u + 1) * H // 2])
+        crosses.append(load_list(cross3, "c3"))
+        sc_picked = sb([P, S], U8, "sc_picked")
+        nc.vector.tensor_copy(sc_picked[:], scale_table[:].indirect(users[:]))
+        for r in range(4):
+            nc.sync.dma_start(x_sc[r:P:32, :].bitcast(I32), sc_picked[SCALE_ROW0 + r : P : 4, :].bitcast(I32))
+        word_table = placed([P, T], I32, "word_table", 4096)
+        nc.sync.dma_start(word_table[:], x_words[0].rearrange("p n t -> p (n t)").bitcast(I32))
+        w2_raw = placed([P, PACK, N], F32, "w2_raw", 0)
+        nc.sync.dma_start(w2_raw[:], w2.rearrange("(p j) c -> p j c", j=PACK))
+
+        looked = [[sb([P, S], F32, "looked0_%d" % i) for i in range(3)], [placed([P, S], F32, "looked1_0", 16384), sb([P, S], F32, "looked1_1"), sb([P, S], F32, "looked1_2")]]
+        nc.vector.tensor_copy(looked[0][0][:], wide_rows[0][:].indirect(crosses[0][:]))
+        for b, i in [(0, 1), (1, 0), (1, 1), (0, 2), (1, 2)]:
+            nc.scalar.activation(looked[b][i][:], wide_rows[b][:].indirect(crosses[i][:]), COPY)
+
+        w1_bf = sb([P, H * PACK], BF16, "w1_bf")
+        w1_dst = w1_bf[:].rearrange("p (t m j) -> p m j t", t=PACK, j=PACK)
+        pair0 = sb([P, S], F32, "pair0")
+        nc.vector.tensor_tensor(pair0[:], looked[0][0][:], looked[0][1][:], ADD)
+        nc.vector.tensor_copy(w1_dst[:, 0 : P // 2], w1_raw[0][:].rearrange("p j (m t) -> p m j t", t=PACK))
+        for e in range(2):
             nc.vector.tensor_copy(
-                x_codes[:, u * HALF : (u + 1) * HALF],
-                word_table[:].bitcast(U32).indirect(users[:, u * HALF // 16 : (u + 1) * HALF // 16]),
+                w1_dst[:, (2 + e) * P // 4 : (3 + e) * P // 4],
+                w1_raw[1][:, :, e * P : (e + 1) * P].rearrange("p j (m t) -> p m j t", t=PACK),
             )
 
-        w2_bf = sb([P, N * PACK], BF16, "w2_bf")
-        w2_dst = w2_bf[:].rearrange("p (c i j) -> p c j i", i=4, j=PACK)
-        w2_src = w2_raw[:].rearrange("p j (c i) -> p c j i", i=4)
-        nc.scalar.activation(w2_dst[:, 0:32], w2_src[:, 0:32], COPY)
-        nc.vector.tensor_copy(w2_dst[:, 32:64], w2_src[:, 32:64])
-        w2_mx = quantise(w2_bf, N, "w2")
+        def runs(t):
+            return t[:].rearrange("p (j c) -> p j c", j=PACK)
 
-        h_bf = [reuse.tile([P, HALF * PACK], BF16, name="h_bf%d" % u, align_bytes=64, offset=u * 2048) for u in range(2)]
-        early = [sb([P, S], F32, "early%d" % i) for i in range(2)]
-        zeros = [0.0, early[1][:, 0:1], 0.0, early[1][:, HALF : HALF + 1]]
-        for z in zeros[1::2]:
-            nc.gpsimd.memset(z, 0.0)
+        pair1 = w1_raw[1][:, :, 0:P]
+        nc.vector.tensor_tensor(pair1, runs(looked[1][0]), runs(looked[1][1]), ADD)
+        w1_mx = quantise(w1_bf, H, "w1")
+        wide_sum = [placed([P, S], F32, "wide_sum0", 16384), placed([P, S], F32, "wide_sum1", 0)]
+        nc.vector.tensor_tensor(wide_sum[0][:], pair0[:], looked[0][2][:], ADD)
+
+        x_codes = [sb([P, P], U32, "x_codes%d" % c) for c in range(S // P)]
+        for c in range(S // P):
+            nc.vector.tensor_copy(x_codes[c][:], word_table[:].bitcast(U32).indirect(users[:, c * P // 16 : (c + 1) * P // 16]))
+
+        h_bf = [sb([P, HALF * PACK], BF16, "h_bf%d" % u) for u in range(2)]
         for c in range(S // P):
             u, e = divmod(c, 2)
-            bank = psum.tile([P, PACK, P], F32, name="hbank%d" % c, tag="bank%d" % c)
+            bank = psum.tile([P, PACK, P], F32, name="hbank%d" % c)
             for t in range(PACK):
-                product(bank[:, t, :], w1_mx, slice(t * P, (t + 1) * P), (x_codes, x_sc), slice(c * P, (c + 1) * P))
+                product(bank[:, t, :], w1_mx, slice(t * P, (t + 1) * P), (x_codes[c], x_sc[:, c * P : (c + 1) * P]), slice(0, P))
             nc.scalar.activation(
                 h_bf[u][:, e * P * PACK : (e + 1) * P * PACK].rearrange("p (n t) -> p n t", t=PACK),
                 bank[:].rearrange("p t n -> p n t"),
                 RELU,
-                bias=zeros[c],
+                bias=relu_bias[:],
             )
 
-        def products(u):
-            h_mx = quantise(h_bf[u], HALF, "h%d" % u)
-            y0t = psum.tile([P, 2, P], F32, name="y0t_%d" % u)
-            y1 = psum.tile([P, HALF], F32, name="y1_%d" % u, tag="bank%d" % (2 * u))
-            for e in range(2):
-                product(y0t[:, e, :], h_mx, slice(e * P, (e + 1) * P), w2_mx, slice(0, P))
-            product(y1[:], w2_mx, slice(P, 2 * P), h_mx, slice(0, HALF))
-            return y0t, y1
-
-        def finish_block0(u, y0t):
-            y0t_sb = sb([P, HALF], F32, "y0t_sb%d" % u)
-            nc.scalar.copy(y0t_sb[:], y0t[:].rearrange("p e n -> p (e n)"))
-            back = psum.tile([P, 2, P], F32, name="back%d" % u, tag="bank%d" % (2 * u + 1))
-            turn(back, [columns(turned0_sb, u * HALF), columns(y0t_sb)])
-            res = sb([P, HALF], F32, "res0_%d" % u)
-            nc.scalar.copy(res[:], back[:].rearrange("p e n -> p (e n)"))
-            nc.scalar.dma_start(out[0:P, u * HALF : (u + 1) * HALF], res[:])
-
-        nc.vector.tensor_copy(early[0][:], picked(1, 0, 0, S))
-        y0t_lo, y1_lo = products(0)
-        nc.vector.tensor_tensor(early[1][:, 0:HALF], picked(1, 1, 0, HALF), early[0][:, 0:HALF], ADD)
-        y0t_hi, y1_hi = products(1)
-        nc.vector.tensor_tensor(early[1][:, HALF:S], picked(1, 1, HALF, HALF), early[0][:, HALF:S], ADD)
-        summed = [reuse.tile([P, HALF], F32, name="summed0", align_bytes=64, offset=2048), sb([P, HALF], F32, "summed1")]
+        w2_bf = sb([P, N * PACK], BF16, "w2_bf")
+        nc.vector.tensor_copy(
+            w2_bf[:].rearrange("p (c i j) -> p c j i", i=4, j=PACK),
+            w2_raw[:].rearrange("p j (c i) -> p c j i", i=4),
+        )
+        nc.vector.tensor_tensor(runs(wide_sum[1]), pair1, runs(looked[1][2]), ADD)
+        w2_mx = quantise(w2_bf, N, "w2")
+        h_mx = [quantise(h_bf[u], HALF, "h%d" % u) for u in range(2)]
         for u in range(2):
             cols = slice(u * HALF, (u + 1) * HALF)
-            nc.vector.tensor_tensor(summed[u][:], picked(1, 2, u * HALF, HALF), early[1][:, cols], ADD)
-        for u, y1 in enumerate((y1_lo, y1_hi)):
-            cols = slice(u * HALF, (u + 1) * HALF)
-            res = sb([P, HALF], F32, "res1_%d" % u)
-            nc.vector.tensor_tensor(res[:], y1[:], summed[u][:], ADD)
-            nc.sync.dma_start(out[P : 2 * P, cols], res[:])
-        finish_block0(0, y0t_lo)
-        finish_block0(1, y0t_hi)
+            for b in range(2):
+                y = psum.tile([P, HALF], F32, name="y%d_%d" % (b, u))
+                product(y[:], w2_mx, slice(b * P, (b + 1) * P), h_mx[u], slice(0, HALF))
+                res = sb([P, HALF], F32, "res%d_%d" % (b, u))
+                nc.vector.tensor_tensor(res[:], y[:], wide_sum[b][:, cols], ADD)
+                nc.sync.dma_start(out[b * P : (b + 1) * P, cols], res[:])

@@ -70,12 +70,10 @@ def tile_picked_ywide_none_p_kernel(tc, x_words, x_scales, w1, w2, wide, offs, c
 
         wide_rows = [sb([P, R], F32, "wide%d" % b) for b in range(2)]
         nc.sync.dma_start(wide_rows[0][:], wide[0:P, :])
-        crosses = [load_list(cross1, "c1"), load_list(cross2, "c2")]
+        crosses = [load_list(cross1, "c1"), load_list(cross2, "c2"), load_list(cross3, "c3")]
         nc.sync.dma_start(wide_rows[1][:], wide[P : 2 * P, :])
-        w1_raw = [sb([P, PACK, H // 2], F32, "w1_raw%d" % u) for u in range(2)]
-        for u in range(2):
-            nc.sync.dma_start(w1_raw[u][:], w1.rearrange("(p j) c -> p j c", j=PACK)[:, :, u * H // 2 : (u + 1) * H // 2])
-        crosses.append(load_list(cross3, "c3"))
+        w1_raw = placed([P, PACK, H], F32, "w1_raw", 12288)
+        nc.sync.dma_start(w1_raw[:], w1.rearrange("(p j) c -> p j c", j=PACK))
         sc_picked = sb([P, S], U8, "sc_picked")
         nc.vector.tensor_copy(sc_picked[:], scale_table[:].indirect(users[:]))
         for r in range(4):
@@ -85,30 +83,25 @@ def tile_picked_ywide_none_p_kernel(tc, x_words, x_scales, w1, w2, wide, offs, c
         w2_raw = placed([P, PACK, N], F32, "w2_raw", 0)
         nc.sync.dma_start(w2_raw[:], w2.rearrange("(p j) c -> p j c", j=PACK))
 
-        looked = [[sb([P, S], F32, "looked0_%d" % i) for i in range(3)], [placed([P, S], F32, "looked1_0", 16384), sb([P, S], F32, "looked1_1"), sb([P, S], F32, "looked1_2")]]
-        nc.vector.tensor_copy(looked[0][0][:], wide_rows[0][:].indirect(crosses[0][:]))
-        for b, i in [(0, 1), (1, 0), (1, 1), (0, 2), (1, 2)]:
+        looked = [[sb([P, S], F32, "looked%d_%d" % (b, i)) for i in range(3 - b)] for b in range(2)]
+        for i in (0, 2):
+            nc.vector.tensor_copy(looked[0][i][:], wide_rows[0][:].indirect(crosses[i][:]))
+        for b, i in [(0, 1), (1, 0), (1, 1)]:
             nc.scalar.activation(looked[b][i][:], wide_rows[b][:].indirect(crosses[i][:]), COPY)
+        pair = [sb([P, S], F32, "pair%d" % b) for b in range(2)]
+        wide_sum = [sb([P, S], F32, "wide_sum0"), placed([P, S], F32, "wide_sum1", 0)]
+        nc.vector.tensor_tensor(pair[0][:], looked[0][0][:], looked[0][1][:], ADD)
+        nc.vector.tensor_tensor(wide_sum[0][:], pair[0][:], looked[0][2][:], ADD)
+        nc.vector.tensor_tensor(pair[1][:], looked[1][0][:], looked[1][1][:], ADD)
 
         w1_bf = sb([P, H * PACK], BF16, "w1_bf")
         w1_dst = w1_bf[:].rearrange("p (t m j) -> p m j t", t=PACK, j=PACK)
-        pair0 = sb([P, S], F32, "pair0")
-        nc.vector.tensor_tensor(pair0[:], looked[0][0][:], looked[0][1][:], ADD)
-        nc.vector.tensor_copy(w1_dst[:, 0 : P // 2], w1_raw[0][:].rearrange("p j (m t) -> p m j t", t=PACK))
-        for e in range(2):
-            nc.vector.tensor_copy(
-                w1_dst[:, (2 + e) * P // 4 : (3 + e) * P // 4],
-                w1_raw[1][:, :, e * P : (e + 1) * P].rearrange("p j (m t) -> p m j t", t=PACK),
-            )
-
-        def runs(t):
-            return t[:].rearrange("p (j c) -> p j c", j=PACK)
-
-        pair1 = w1_raw[1][:, :, 0:P]
-        nc.vector.tensor_tensor(pair1, runs(looked[1][0]), runs(looked[1][1]), ADD)
+        w1_src = w1_raw[:].rearrange("p j (m t) -> p m j t", t=PACK)
+        nc.vector.tensor_copy(w1_dst[:, 0 : P // 2], w1_src[:, 0 : P // 2])
+        nc.scalar.activation(w1_dst[:, P // 2 : P], w1_src[:, P // 2 : P], COPY)
+        last_looked = placed([P, S], F32, "looked1_2", 12288)
+        nc.scalar.activation(last_looked[:], wide_rows[1][:].indirect(crosses[2][:]), COPY)
         w1_mx = quantise(w1_bf, H, "w1")
-        wide_sum = [placed([P, S], F32, "wide_sum0", 16384), placed([P, S], F32, "wide_sum1", 0)]
-        nc.vector.tensor_tensor(wide_sum[0][:], pair0[:], looked[0][2][:], ADD)
 
         x_codes = [sb([P, P], U32, "x_codes%d" % c) for c in range(S // P)]
         for c in range(S // P):
@@ -132,7 +125,7 @@ def tile_picked_ywide_none_p_kernel(tc, x_words, x_scales, w1, w2, wide, offs, c
             w2_bf[:].rearrange("p (c i j) -> p c j i", i=4, j=PACK),
             w2_raw[:].rearrange("p j (c i) -> p c j i", i=4),
         )
-        nc.vector.tensor_tensor(runs(wide_sum[1]), pair1, runs(looked[1][2]), ADD)
+        nc.vector.tensor_tensor(wide_sum[1][:], pair[1][:], last_looked[:], ADD)
         w2_mx = quantise(w2_bf, N, "w2")
         h_mx = [quantise(h_bf[u], HALF, "h%d" % u) for u in range(2)]
         for u in range(2):

@@ -72,7 +72,7 @@ def tile_picked_ywide_none_p_kernel(tc, x_words, x_scales, w1, w2, wide, offs, c
         nc.sync.dma_start(wide_rows[0][:], wide[0:P, :])
         crosses = [load_list(cross1, "c1"), load_list(cross2, "c2"), load_list(cross3, "c3")]
         nc.sync.dma_start(wide_rows[1][:], wide[P : 2 * P, :])
-        w1_raw = placed([P, PACK, H], F32, "w1_raw", 12288)
+        w1_raw = sb([P, PACK, H], F32, "w1_raw")
         nc.sync.dma_start(w1_raw[:], w1.rearrange("(p j) c -> p j c", j=PACK))
         sc_picked = sb([P, S], U8, "sc_picked")
         nc.vector.tensor_copy(sc_picked[:], scale_table[:].indirect(users[:]))
@@ -83,24 +83,25 @@ def tile_picked_ywide_none_p_kernel(tc, x_words, x_scales, w1, w2, wide, offs, c
         w2_raw = placed([P, PACK, N], F32, "w2_raw", 0)
         nc.sync.dma_start(w2_raw[:], w2.rearrange("(p j) c -> p j c", j=PACK))
 
-        looked = [[sb([P, S], F32, "looked%d_%d" % (b, i)) for i in range(3 - b)] for b in range(2)]
+        looked = [[sb([P, S], F32, "looked%d_%d" % (b, i)) for i in range(3)] for b in range(2)]
         for i in (0, 2):
             nc.vector.tensor_copy(looked[0][i][:], wide_rows[0][:].indirect(crosses[i][:]))
-        for b, i in [(0, 1), (1, 0), (1, 1)]:
+        for b, i in [(0, 1), (1, 0), (1, 1), (1, 2)]:
             nc.scalar.activation(looked[b][i][:], wide_rows[b][:].indirect(crosses[i][:]), COPY)
-        pair = [sb([P, S], F32, "pair%d" % b) for b in range(2)]
-        wide_sum = [sb([P, S], F32, "wide_sum0"), placed([P, S], F32, "wide_sum1", 0)]
-        nc.vector.tensor_tensor(pair[0][:], looked[0][0][:], looked[0][1][:], ADD)
-        nc.vector.tensor_tensor(wide_sum[0][:], pair[0][:], looked[0][2][:], ADD)
-        nc.vector.tensor_tensor(pair[1][:], looked[1][0][:], looked[1][1][:], ADD)
+        pair0 = sb([P, S], F32, "pair0")
+        nc.vector.tensor_tensor(pair0[:], looked[0][0][:], looked[0][1][:], ADD)
 
         w1_bf = sb([P, H * PACK], BF16, "w1_bf")
         w1_dst = w1_bf[:].rearrange("p (t m j) -> p m j t", t=PACK, j=PACK)
         w1_src = w1_raw[:].rearrange("p j (m t) -> p m j t", t=PACK)
-        nc.vector.tensor_copy(w1_dst[:, 0 : P // 2], w1_src[:, 0 : P // 2])
-        nc.scalar.activation(w1_dst[:, P // 2 : P], w1_src[:, P // 2 : P], COPY)
-        last_looked = placed([P, S], F32, "looked1_2", 12288)
-        nc.scalar.activation(last_looked[:], wide_rows[1][:].indirect(crosses[2][:]), COPY)
+        for u in range(2):
+            nc.vector.tensor_copy(w1_dst[:, u * P // 2 : (u + 1) * P // 2], w1_src[:, u * P // 2 : (u + 1) * P // 2])
+
+        def halves(t):
+            return t[:].rearrange("p (u c) -> p u c", u=2)
+
+        sum0 = w1_raw[:, 0:2, 0:HALF]
+        nc.vector.tensor_tensor(sum0, halves(pair0), halves(looked[0][2]), ADD)
         w1_mx = quantise(w1_bf, H, "w1")
 
         x_codes = [sb([P, P], U32, "x_codes%d" % c) for c in range(S // P)]
@@ -120,19 +121,24 @@ def tile_picked_ywide_none_p_kernel(tc, x_words, x_scales, w1, w2, wide, offs, c
                 bias=relu_bias[:],
             )
 
-        w2_bf = sb([P, N * PACK], BF16, "w2_bf")
+        w2_bf = placed([P, N * PACK], BF16, "w2_bf", 12288)
         nc.vector.tensor_copy(
             w2_bf[:].rearrange("p (c i j) -> p c j i", i=4, j=PACK),
             w2_raw[:].rearrange("p j (c i) -> p c j i", i=4),
         )
-        nc.vector.tensor_tensor(wide_sum[1][:], pair[1][:], last_looked[:], ADD)
+        pair1 = placed([P, S], F32, "pair1", 0)
+        nc.vector.tensor_tensor(pair1[:], looked[1][0][:], looked[1][1][:], ADD)
         w2_mx = quantise(w2_bf, N, "w2")
-        h_mx = [quantise(h_bf[u], HALF, "h%d" % u) for u in range(2)]
+        h_mx = [quantise(h_bf[0], HALF, "h0")]
+        sum1 = placed([P, S], F32, "sum1", 12288)
+        nc.vector.tensor_tensor(sum1[:], pair1[:], looked[1][2][:], ADD)
+        h_mx.append(quantise(h_bf[1], HALF, "h1"))
+        wide_sum = [sum0, halves(sum1)]
         for u in range(2):
             cols = slice(u * HALF, (u + 1) * HALF)
             for b in range(2):
                 y = psum.tile([P, HALF], F32, name="y%d_%d" % (b, u))
                 product(y[:], w2_mx, slice(b * P, (b + 1) * P), h_mx[u], slice(0, HALF))
                 res = sb([P, HALF], F32, "res%d_%d" % (b, u))
-                nc.vector.tensor_tensor(res[:], y[:], wide_sum[b][:, cols], ADD)
+                nc.vector.tensor_tensor(res[:], y[:], wide_sum[b][:, u, :], ADD)
                 nc.sync.dma_start(out[b * P : (b + 1) * P, cols], res[:])

@@ -89,20 +89,22 @@ def tile_picked_ywide_none_p_kernel(tc, x_words, x_scales, w1, w2, wide, offs, c
         for b, i in [(0, 1), (1, 0), (1, 1), (1, 2)]:
             nc.scalar.activation(looked[b][i][:], wide_rows[b][:].indirect(crosses[i][:]), COPY)
         pair0 = sb([P, S], F32, "pair0")
-        nc.vector.tensor_tensor(pair0[:], looked[0][0][:], looked[0][1][:], ADD)
+        sum0 = sb([P, S], F32, "sum0")
+        for u in range(2):
+            cols = slice(u * HALF, (u + 1) * HALF)
+            nc.vector.tensor_tensor(pair0[:, cols], looked[0][0][:, cols], looked[0][1][:, cols], ADD)
+        for u in range(2):
+            cols = slice(u * HALF, (u + 1) * HALF)
+            nc.vector.tensor_tensor(sum0[:, cols], pair0[:, cols], looked[0][2][:, cols], ADD)
 
-        w1_bf = sb([P, H * PACK], BF16, "w1_bf")
-        w1_dst = w1_bf[:].rearrange("p (t m j) -> p m j t", t=PACK, j=PACK)
+        w1_bf = [sb([P, H * PACK // 2], BF16, "w1_bf%d" % u) for u in range(2)]
         w1_src = w1_raw[:].rearrange("p j (m t) -> p m j t", t=PACK)
         for u in range(2):
-            nc.vector.tensor_copy(w1_dst[:, u * P // 2 : (u + 1) * P // 2], w1_src[:, u * P // 2 : (u + 1) * P // 2])
+            nc.vector.tensor_copy(w1_bf[u][:].rearrange("p (t m j) -> p m j t", t=2, j=PACK), w1_src[:, :, :, 2 * u : 2 * u + 2])
+        w1_mx = [quantise(w1_bf[u], H // 2, "w1_%d" % u) for u in range(2)]
 
         def halves(t):
             return t[:].rearrange("p (u c) -> p u c", u=2)
-
-        sum0 = w1_raw[:, 0:2, 0:HALF]
-        nc.vector.tensor_tensor(sum0, halves(pair0), halves(looked[0][2]), ADD)
-        w1_mx = quantise(w1_bf, H, "w1")
 
         x_codes = [sb([P, P], U32, "x_codes%d" % c) for c in range(S // P)]
         for c in range(S // P):
@@ -113,7 +115,7 @@ def tile_picked_ywide_none_p_kernel(tc, x_words, x_scales, w1, w2, wide, offs, c
             u, e = divmod(c, 2)
             bank = psum.tile([P, PACK, P], F32, name="hbank%d" % c)
             for t in range(PACK):
-                product(bank[:, t, :], w1_mx, slice(t * P, (t + 1) * P), (x_codes[c], x_sc[:, c * P : (c + 1) * P]), slice(0, P))
+                product(bank[:, t, :], w1_mx[t // 2], slice(t % 2 * P, (t % 2 + 1) * P), (x_codes[c], x_sc[:, c * P : (c + 1) * P]), slice(0, P))
             nc.scalar.activation(
                 h_bf[u][:, e * P * PACK : (e + 1) * P * PACK].rearrange("p (n t) -> p n t", t=PACK),
                 bank[:].rearrange("p t n -> p n t"),
@@ -133,7 +135,7 @@ def tile_picked_ywide_none_p_kernel(tc, x_words, x_scales, w1, w2, wide, offs, c
         sum1 = placed([P, S], F32, "sum1", 12288)
         nc.vector.tensor_tensor(sum1[:], pair1[:], looked[1][2][:], ADD)
         h_mx.append(quantise(h_bf[1], HALF, "h1"))
-        wide_sum = [sum0, halves(sum1)]
+        wide_sum = [halves(sum0), halves(sum1)]
         for u in range(2):
             cols = slice(u * HALF, (u + 1) * HALF)
             for b in range(2):

@@ -1,6 +1,7 @@
 from contextlib import ExitStack
 
 import concourse.mybir as mybir
+from concourse.masks import make_identity
 
 F32 = mybir.dt.float32
 BF16 = mybir.dt.bfloat16
@@ -11,6 +12,7 @@ U8 = mybir.dt.uint8
 FP8X4 = mybir.dt.float8_e4m3fn_x4
 ADD = mybir.AluOpType.add
 COPY = mybir.ActivationFunctionType.Copy
+IDENTITY = mybir.ActivationFunctionType.Identity
 RELU = mybir.ActivationFunctionType.Relu
 
 K, T, S, H, N, R = 512, 2048, 512, 512, 256, 1024
@@ -40,8 +42,8 @@ def tile_picked_ywide_none_p_kernel(tc, x_words, x_scales, w1, w2, wide, offs, c
             nc.sync.dma_start(t[:], src)
             return t
 
-        def quantise(src, width, name):
-            codes = sb([P, width], U32, name + "_codes")
+        def quantise(src, width, name, offset=None):
+            codes = sb([P, width], U32, name + "_codes") if offset is None else placed([P, width], U32, name + "_codes", offset)
             scales = sb([P, width], U8, name + "_sc")
             nc.vector.quantize_mx(out=codes[:].bitcast(FP8X4), scales=scales[:], in_=src[:])
             return codes, scales
@@ -61,12 +63,15 @@ def tile_picked_ywide_none_p_kernel(tc, x_words, x_scales, w1, w2, wide, offs, c
         nc.scalar.dma_start(scale_table[SCALE_ROW0:P, :].bitcast(I32), x_scales[0].bitcast(I32))
         users = load_list(offs, "users")
         nc.vector.memset(scale_table[0:SCALE_ROW0, :].bitcast(I32), 0)
-        zero_seed = sb([P, 1], F32, "zero_seed")
-        nc.gpsimd.memset(zero_seed[:], 0.0)
+        last_looked = sb([P, S], F32, "looked1_2")
+        nc.gpsimd.memset(last_looked[:, 0:1], 0.0)
         relu_bias = sb([P, 1], F32, "relu_bias")
-        nc.scalar.activation(relu_bias[:], zero_seed[:], COPY)
+        nc.scalar.activation(relu_bias[:], last_looked[:, 0:1], COPY)
         x_sc = sb([P, S], U8, "x_sc")
         nc.gpsimd.memset(x_sc[:].bitcast(I32), 0)
+
+        ident = sb([P, P], F32, "ident")
+        make_identity(nc, ident[:])
 
         wide_rows = [sb([P, R], F32, "wide%d" % b) for b in range(2)]
         nc.sync.dma_start(wide_rows[0][:], wide[0:P, :])
@@ -83,64 +88,88 @@ def tile_picked_ywide_none_p_kernel(tc, x_words, x_scales, w1, w2, wide, offs, c
         w2_raw = placed([P, PACK, N], F32, "w2_raw", 0)
         nc.sync.dma_start(w2_raw[:], w2.rearrange("(p j) c -> p j c", j=PACK))
 
-        looked = [[sb([P, S], F32, "looked%d_%d" % (b, i)) for i in range(3)] for b in range(2)]
-        for i in (0, 2):
-            nc.vector.tensor_copy(looked[0][i][:], wide_rows[0][:].indirect(crosses[i][:]))
-        for b, i in [(0, 1), (1, 0), (1, 1), (1, 2)]:
+        shared = sb([P, 2 * S], F32, "shared")
+        wide_sum = shared[:].rearrange("p (b n) -> p b n", b=2)
+        nc.gpsimd.memset(shared[:, 0:1], 1.0)
+        back_bias = placed([P, 544], F32, "back_bias", 20480 + 1024 - 64)
+        nc.gpsimd.memset(back_bias[:, 0:1], 0.0)
+
+        looked = [[sb([P, S], F32, "looked%d_%d" % (b, i)) for i in range(3 - b)] for b in range(2)]
+        for b, i in [(0, 0), (0, 1), (1, 0)]:
+            nc.vector.tensor_copy(looked[b][i][:], wide_rows[b][:].indirect(crosses[i][:]))
+        for b, i in [(0, 2), (1, 1)]:
             nc.scalar.activation(looked[b][i][:], wide_rows[b][:].indirect(crosses[i][:]), COPY)
-        pair0 = sb([P, S], F32, "pair0")
-        sum0 = sb([P, S], F32, "sum0")
-        for u in range(2):
-            cols = slice(u * HALF, (u + 1) * HALF)
-            nc.vector.tensor_tensor(pair0[:, cols], looked[0][0][:, cols], looked[0][1][:, cols], ADD)
-        for u in range(2):
-            cols = slice(u * HALF, (u + 1) * HALF)
-            nc.vector.tensor_tensor(sum0[:, cols], pair0[:, cols], looked[0][2][:, cols], ADD)
 
-        w1_bf = [sb([P, H * PACK // 2], BF16, "w1_bf%d" % u) for u in range(2)]
+        def turn(name, sources):
+            dst = psum.tile([P, S // P, P], F32, name=name, tag=name)
+            for k, src in enumerate(sources):
+                for c in range(S // P):
+                    nc.tensor.matmul(
+                        dst[:, c, :], src[:, c * P : (c + 1) * P], ident[:],
+                        start=(k == 0 and c == 0), stop=(k == len(sources) - 1 and c == S // P - 1), is_transpose=True,
+                    )
+            return dst[:].rearrange("p c n -> p (c n)")
+
+        turned = sb([P, S], F32, "turned")
+        nc.scalar.activation(turned[:], turn("y0", [looked[0][0], looked[0][2], looked[0][1]]), IDENTITY, bias=last_looked[:, 0:1])
+        turned_back = turn("y1", [turned])
+
+        w1_bf = sb([P, H * PACK], BF16, "w1_bf")
+        w1_dst = w1_bf[:].rearrange("p (t m j) -> p m j t", t=PACK, j=PACK)
         w1_src = w1_raw[:].rearrange("p j (m t) -> p m j t", t=PACK)
-        for u in range(2):
-            nc.vector.tensor_copy(w1_bf[u][:].rearrange("p (t m j) -> p m j t", t=2, j=PACK), w1_src[:, :, :, 2 * u : 2 * u + 2])
-        w1_mx = [quantise(w1_bf[u], H // 2, "w1_%d" % u) for u in range(2)]
+        nc.vector.tensor_copy(w1_dst[:, 0:32], w1_src[:, 0:32])
+        nc.vector.tensor_copy(w1_dst[:, 32:96], w1_src[:, 32:96])
+        nc.scalar.activation(w1_dst[:, 96:P], w1_src[:, 96:P], IDENTITY, bias=last_looked[:, 0:1], scale=shared[:, 0:1])
+        nc.scalar.activation(last_looked[:], wide_rows[1][:].indirect(crosses[2][:]), COPY)
+        nc.scalar.activation(wide_sum[:, 0, :], turned_back, IDENTITY, bias=back_bias[:, 0:1])
 
-        def halves(t):
-            return t[:].rearrange("p (u c) -> p u c", u=2)
+        def runs(t):
+            return t[:].rearrange("p (j c) -> p j c", j=PACK)
 
-        x_codes = [sb([P, P], U32, "x_codes%d" % c) for c in range(S // P)]
-        for c in range(S // P):
-            nc.vector.tensor_copy(x_codes[c][:], word_table[:].bitcast(U32).indirect(users[:, c * P // 16 : (c + 1) * P // 16]))
+        pair1 = w1_raw[:, :, 0:P]
+        nc.vector.tensor_tensor(pair1, runs(looked[1][0]), runs(looked[1][1]), ADD)
+        w1_mx = quantise(w1_bf, H, "w1")
 
-        h_bf = [sb([P, HALF * PACK], BF16, "h_bf%d" % u) for u in range(2)]
-        for c in range(S // P):
-            u, e = divmod(c, 2)
+        pieces = [(0, P), (P, P), (HALF, HALF)]
+        x_codes = []
+        for first, width in pieces:
+            picked = sb([P, width], U32, "x_codes%d" % first)
+            nc.vector.tensor_copy(picked[:], word_table[:].bitcast(U32).indirect(users[:, first // 16 : (first + width) // 16]))
+            x_codes.extend(picked[:, e * P : (e + 1) * P] for e in range(width // P))
+
+        chunks = S // P
+        h_bf = [placed([P, P * PACK], BF16, "h_bf%d" % c, 20480 + 1024 * c) for c in range(chunks)]
+        for c in range(chunks):
             bank = psum.tile([P, PACK, P], F32, name="hbank%d" % c)
             for t in range(PACK):
-                product(bank[:, t, :], w1_mx[t // 2], slice(t % 2 * P, (t % 2 + 1) * P), (x_codes[c], x_sc[:, c * P : (c + 1) * P]), slice(0, P))
+                product(bank[:, t, :], w1_mx, slice(t * P, (t + 1) * P), (x_codes[c], x_sc[:, c * P : (c + 1) * P]), slice(0, P))
             nc.scalar.activation(
-                h_bf[u][:, e * P * PACK : (e + 1) * P * PACK].rearrange("p (n t) -> p n t", t=PACK),
+                h_bf[c][:].rearrange("p (n t) -> p n t", t=PACK),
                 bank[:].rearrange("p t n -> p n t"),
                 RELU,
                 bias=relu_bias[:],
             )
 
-        w2_bf = placed([P, N * PACK], BF16, "w2_bf", 12288)
-        nc.vector.tensor_copy(
-            w2_bf[:].rearrange("p (c i j) -> p c j i", i=4, j=PACK),
-            w2_raw[:].rearrange("p j (c i) -> p c j i", i=4),
-        )
-        pair1 = placed([P, S], F32, "pair1", 0)
-        nc.vector.tensor_tensor(pair1[:], looked[1][0][:], looked[1][1][:], ADD)
+        w2_bf = shared[:, S : 2 * S].bitcast(BF16)
+        nc.vector.tensor_copy(w2_bf.rearrange("p (c i j) -> p c j i", i=4, j=PACK), w2_raw[:].rearrange("p j (c i) -> p c j i", i=4))
         w2_mx = quantise(w2_bf, N, "w2")
-        h_mx = [quantise(h_bf[0], HALF, "h0")]
-        sum1 = placed([P, S], F32, "sum1", 12288)
-        nc.vector.tensor_tensor(sum1[:], pair1[:], looked[1][2][:], ADD)
-        h_mx.append(quantise(h_bf[1], HALF, "h1"))
-        wide_sum = [halves(sum0), halves(sum1)]
-        for u in range(2):
-            cols = slice(u * HALF, (u + 1) * HALF)
+        nc.vector.tensor_tensor(runs(wide_sum[:, 1, :]), pair1, runs(last_looked), ADD)
+        out_rows = out.rearrange("(b p) n -> p b n", p=P)
+
+        def products(c, h_mx):
+            y = psum.tile([P, 2, P], F32, name="product%d" % c, tag="y%d" % c)
             for b in range(2):
-                y = psum.tile([P, HALF], F32, name="y%d_%d" % (b, u))
-                product(y[:], w2_mx, slice(b * P, (b + 1) * P), h_mx[u], slice(0, HALF))
-                res = sb([P, HALF], F32, "res%d_%d" % (b, u))
-                nc.vector.tensor_tensor(res[:], y[:], wide_sum[b][:, u, :], ADD)
-                nc.sync.dma_start(out[b * P : (b + 1) * P, cols], res[:])
+                product(y[:, b, :], w2_mx, slice(b * P, (b + 1) * P), h_mx, slice(0, P))
+            return y
+
+        def finish(c, y, res):
+            cols = slice(c * P, (c + 1) * P)
+            nc.vector.tensor_tensor(res[:], y[:], wide_sum[:, :, cols], ADD)
+            nc.sync.dma_start(out_rows[:, :, cols], res[:])
+
+        y = [products(c, quantise(h_bf[c], P, "h%d" % c, 512 * c)) for c in range(chunks - 1)]
+        res = [sb([P, 2, P], F32, "res%d" % c) for c in range(chunks)]
+        finish(0, y[0], res[0])
+        y.append(products(3, quantise(h_bf[3], P, "h3", 0)))
+        for c in range(1, chunks):
+            finish(c, y[c], res[c])

@@ -12,7 +12,6 @@ U8 = mybir.dt.uint8
 FP8X4 = mybir.dt.float8_e4m3fn_x4
 ADD = mybir.AluOpType.add
 COPY = mybir.ActivationFunctionType.Copy
-IDENTITY = mybir.ActivationFunctionType.Identity
 RELU = mybir.ActivationFunctionType.Relu
 
 K, T, S, H, N, R = 512, 2048, 512, 512, 256, 1024
@@ -21,6 +20,7 @@ PACK = 4
 BLOCKS = K // 32
 SCALE_ROW0 = P - BLOCKS
 HALF = S // 2
+CHUNKS = S // P
 FLOPS = 2 * K * H * S + 2 * H * N * S
 
 
@@ -42,10 +42,13 @@ def tile_picked_ywide_none_p_kernel(tc, x_words, x_scales, w1, w2, wide, offs, c
             nc.sync.dma_start(t[:], src)
             return t
 
+        def entries(lst, first, count):
+            return lst[:, first // 16 : (first + count) // 16]
+
         def quantise(src, width, name, offset=None):
             codes = sb([P, width], U32, name + "_codes") if offset is None else placed([P, width], U32, name + "_codes", offset)
             scales = sb([P, width], U8, name + "_sc")
-            nc.vector.quantize_mx(out=codes[:].bitcast(FP8X4), scales=scales[:], in_=src[:])
+            nc.vector.quantize_mx(out=codes[:].bitcast(FP8X4), scales=scales[:], in_=src)
             return codes, scales
 
         def product(dst, lhs, lcols, rhs, rcols):
@@ -63,10 +66,10 @@ def tile_picked_ywide_none_p_kernel(tc, x_words, x_scales, w1, w2, wide, offs, c
         nc.scalar.dma_start(scale_table[SCALE_ROW0:P, :].bitcast(I32), x_scales[0].bitcast(I32))
         users = load_list(offs, "users")
         nc.vector.memset(scale_table[0:SCALE_ROW0, :].bitcast(I32), 0)
-        last_looked = sb([P, S], F32, "looked1_2")
-        nc.gpsimd.memset(last_looked[:, 0:1], 0.0)
+        zero = sb([P, 1], F32, "zero")
+        nc.gpsimd.memset(zero[:], 0.0)
         relu_bias = sb([P, 1], F32, "relu_bias")
-        nc.scalar.activation(relu_bias[:], last_looked[:, 0:1], COPY)
+        nc.scalar.activation(relu_bias[:], zero[:], COPY)
         x_sc = sb([P, S], U8, "x_sc")
         nc.gpsimd.memset(x_sc[:].bitcast(I32), 0)
 
@@ -75,7 +78,9 @@ def tile_picked_ywide_none_p_kernel(tc, x_words, x_scales, w1, w2, wide, offs, c
 
         wide_rows = [sb([P, R], F32, "wide%d" % b) for b in range(2)]
         nc.sync.dma_start(wide_rows[0][:], wide[0:P, :])
-        crosses = [load_list(cross1, "c1"), load_list(cross2, "c2"), load_list(cross3, "c3")]
+        list1 = load_list(cross1, "list1")
+        list3 = load_list(cross3, "list3")
+        list2 = load_list(cross2, "list2")
         nc.sync.dma_start(wide_rows[1][:], wide[P : 2 * P, :])
         w1_raw = sb([P, PACK, H], F32, "w1_raw")
         nc.sync.dma_start(w1_raw[:], w1.rearrange("(p j) c -> p j c", j=PACK))
@@ -88,61 +93,75 @@ def tile_picked_ywide_none_p_kernel(tc, x_words, x_scales, w1, w2, wide, offs, c
         w2_raw = placed([P, PACK, N], F32, "w2_raw", 0)
         nc.sync.dma_start(w2_raw[:], w2.rearrange("(p j) c -> p j c", j=PACK))
 
-        shared = sb([P, 2 * S], F32, "shared")
-        wide_sum = shared[:].rearrange("p (b n) -> p b n", b=2)
-        nc.gpsimd.memset(shared[:, 0:1], 1.0)
-        back_bias = placed([P, 544], F32, "back_bias", 20480 + 1024 - 64)
-        nc.gpsimd.memset(back_bias[:, 0:1], 0.0)
+        def look_up(on_vector, dst, b, lst, first, count):
+            window = wide_rows[b][:].indirect(entries(lst, first, count))
+            if on_vector:
+                nc.vector.tensor_copy(dst[:], window)
+            else:
+                nc.scalar.activation(dst[:], window, COPY)
+            return [dst[:, e * P : (e + 1) * P] for e in range(count // P)]
 
-        looked = [[sb([P, S], F32, "looked%d_%d" % (b, i)) for i in range(3 - b)] for b in range(2)]
-        for b, i in [(0, 0), (0, 1), (1, 0)]:
-            nc.vector.tensor_copy(looked[b][i][:], wide_rows[b][:].indirect(crosses[i][:]))
-        for b, i in [(0, 2), (1, 1)]:
-            nc.scalar.activation(looked[b][i][:], wide_rows[b][:].indirect(crosses[i][:]), COPY)
-
-        def turn(name, sources):
-            dst = psum.tile([P, S // P, P], F32, name=name, tag=name)
+        def turn(bank, sources):
+            count = len(sources[0])
+            dst = psum.tile([P, count, P], F32, name="turn%d" % bank, tag="bank%d" % bank)
             for k, src in enumerate(sources):
-                for c in range(S // P):
+                for e in range(count):
                     nc.tensor.matmul(
-                        dst[:, c, :], src[:, c * P : (c + 1) * P], ident[:],
-                        start=(k == 0 and c == 0), stop=(k == len(sources) - 1 and c == S // P - 1), is_transpose=True,
+                        dst[:, e, :], src[e], ident[:],
+                        start=(k == 0 and e == 0), stop=(k == len(sources) - 1 and e == count - 1), is_transpose=True,
                     )
-            return dst[:].rearrange("p c n -> p (c n)")
+            return dst[:].rearrange("p e n -> p (e n)")
 
-        turned = sb([P, S], F32, "turned")
-        nc.scalar.activation(turned[:], turn("y0", [looked[0][0], looked[0][2], looked[0][1]]), IDENTITY, bias=last_looked[:, 0:1])
-        turned_back = turn("y1", [turned])
+        def pieces(t, count):
+            return [t[:, e * P : (e + 1) * P] for e in range(count)]
 
-        w1_bf = sb([P, H * PACK], BF16, "w1_bf")
-        w1_dst = w1_bf[:].rearrange("p (t m j) -> p m j t", t=PACK, j=PACK)
+        g01 = look_up(True, sb([P, S], F32, "g01"), 0, list1, 0, S)
+        g03 = look_up(False, sb([P, S], F32, "g03"), 0, list3, 0, S)
+        g02 = look_up(True, sb([P, P], F32, "g02a"), 0, list2, 0, P)
+        g02 = g02 + look_up(False, sb([P, S - P], F32, "g02b"), 0, list2, P, S - P)
+        g11b = sb([P, HALF], F32, "g11b")
+        look_up(True, g11b, 1, list1, HALF, HALF)
+        g11a = look_up(True, sb([P, HALF], F32, "g11a"), 1, list1, 0, HALF)
+        pair = sb([P, HALF], F32, "pair")
+        nc.vector.tensor_tensor(pair[:], wide_rows[1][:].indirect(entries(list2, HALF, HALF)), g11b[:], ADD)
+        g13a = look_up(False, sb([P, HALF], F32, "g13a"), 1, list3, 0, HALF)
+        g12a = look_up(False, placed([P, HALF], F32, "g12a", 16384), 1, list2, 0, HALF)
+
+        shared = sb([P, 2 * S + HALF], F32, "shared")
+        sums = shared[:, 0 : 2 * S].rearrange("p (b n) -> p b n", b=2)
+        forth0 = turn(0, [g01, g03, g02])
+        forth1 = turn(2, [g11a, g13a, g12a])
+        turned0 = sb([P, S], F32, "turned0")
+        nc.scalar.activation(turned0[:], forth0, COPY)
+        turned1 = sb([P, HALF], F32, "turned1")
+        nc.scalar.activation(turned1[:], forth1, COPY)
+        g13b = placed([P, HALF], F32, "g13b", 16384)
+        look_up(False, g13b, 1, list3, HALF, HALF)
+        back0 = turn(1, [pieces(turned0, 4)])
+        back1 = turn(3, [pieces(turned1, 2)])
+        nc.scalar.activation(sums[:, 0, :], back0, COPY)
+        nc.scalar.activation(sums[:, 1, 0:HALF], back1, COPY)
+
         w1_src = w1_raw[:].rearrange("p j (m t) -> p m j t", t=PACK)
-        nc.vector.tensor_copy(w1_dst[:, 0:32], w1_src[:, 0:32])
-        nc.vector.tensor_copy(w1_dst[:, 32:96], w1_src[:, 32:96])
-        nc.scalar.activation(w1_dst[:, 96:P], w1_src[:, 96:P], IDENTITY, bias=last_looked[:, 0:1], scale=shared[:, 0:1])
-        nc.scalar.activation(last_looked[:], wide_rows[1][:].indirect(crosses[2][:]), COPY)
-        nc.scalar.activation(wide_sum[:, 0, :], turned_back, IDENTITY, bias=back_bias[:, 0:1])
+        w1_bf = []
+        for u in range(2):
+            t = sb([P, 2 * P * PACK], BF16, "w1_bf%d" % u)
+            nc.vector.tensor_copy(t[:].rearrange("p (t m j) -> p m j t", t=2, j=PACK), w1_src[:, :, :, 2 * u : 2 * u + 2])
+            w1_bf.append(t)
+        w1_mx = [quantise(w1_bf[u][:], 2 * P, "w1_%d" % u) for u in range(2)]
 
-        def runs(t):
-            return t[:].rearrange("p (j c) -> p j c", j=PACK)
-
-        pair1 = w1_raw[:, :, 0:P]
-        nc.vector.tensor_tensor(pair1, runs(looked[1][0]), runs(looked[1][1]), ADD)
-        w1_mx = quantise(w1_bf, H, "w1")
-
-        pieces = [(0, P), (P, P), (HALF, HALF)]
         x_codes = []
-        for first, width in pieces:
+        for first, width in [(0, P), (P, P), (HALF, HALF)]:
             picked = sb([P, width], U32, "x_codes%d" % first)
-            nc.vector.tensor_copy(picked[:], word_table[:].bitcast(U32).indirect(users[:, first // 16 : (first + width) // 16]))
+            nc.vector.tensor_copy(picked[:], word_table[:].bitcast(U32).indirect(entries(users, first, width)))
             x_codes.extend(picked[:, e * P : (e + 1) * P] for e in range(width // P))
 
-        chunks = S // P
-        h_bf = [placed([P, P * PACK], BF16, "h_bf%d" % c, 20480 + 1024 * c) for c in range(chunks)]
-        for c in range(chunks):
-            bank = psum.tile([P, PACK, P], F32, name="hbank%d" % c)
+        h_bf = [sb([P, P * PACK], BF16, "h_bf%d" % c) for c in range(CHUNKS)]
+        for c in range(CHUNKS):
+            bank = psum.tile([P, PACK, P], F32, name="hidden%d" % c, tag="bank%d" % (4 + c))
             for t in range(PACK):
-                product(bank[:, t, :], w1_mx, slice(t * P, (t + 1) * P), (x_codes[c], x_sc[:, c * P : (c + 1) * P]), slice(0, P))
+                u, e = divmod(t, 2)
+                product(bank[:, t, :], w1_mx[u], slice(e * P, (e + 1) * P), (x_codes[c], x_sc[:, c * P : (c + 1) * P]), slice(0, P))
             nc.scalar.activation(
                 h_bf[c][:].rearrange("p (n t) -> p n t", t=PACK),
                 bank[:].rearrange("p t n -> p n t"),
@@ -150,26 +169,24 @@ def tile_picked_ywide_none_p_kernel(tc, x_words, x_scales, w1, w2, wide, offs, c
                 bias=relu_bias[:],
             )
 
-        w2_bf = shared[:, S : 2 * S].bitcast(BF16)
+        w2_bf = shared[:, S + HALF : 2 * S + HALF].bitcast(BF16)
         nc.vector.tensor_copy(w2_bf.rearrange("p (c i j) -> p c j i", i=4, j=PACK), w2_raw[:].rearrange("p j (c i) -> p c j i", i=4))
+        h_mx = [quantise(h_bf[0][:], P, "h0", 0)]
         w2_mx = quantise(w2_bf, N, "w2")
-        nc.vector.tensor_tensor(runs(wide_sum[:, 1, :]), pair1, runs(last_looked), ADD)
         out_rows = out.rearrange("(b p) n -> p b n", p=P)
 
-        def products(c, h_mx):
-            y = psum.tile([P, 2, P], F32, name="product%d" % c, tag="y%d" % c)
+        def finish(c):
+            y = psum.tile([P, 2, P], F32, name="product%d" % c, tag="bank%d" % c)
             for b in range(2):
-                product(y[:, b, :], w2_mx, slice(b * P, (b + 1) * P), h_mx, slice(0, P))
-            return y
+                product(y[:, b, :], w2_mx, slice(b * P, (b + 1) * P), h_mx[c], slice(0, P))
+            res = sb([P, 2, P], F32, "res%d" % c)
+            nc.vector.tensor_tensor(res[:], y[:], sums[:, :, c * P : (c + 1) * P], ADD)
+            nc.sync.dma_start(out_rows[:, :, c * P : (c + 1) * P], res[:])
 
-        def finish(c, y, res):
-            cols = slice(c * P, (c + 1) * P)
-            nc.vector.tensor_tensor(res[:], y[:], wide_sum[:, :, cols], ADD)
-            nc.sync.dma_start(out_rows[:, :, cols], res[:])
-
-        y = [products(c, quantise(h_bf[c], P, "h%d" % c, 512 * c)) for c in range(chunks - 1)]
-        res = [sb([P, 2, P], F32, "res%d" % c) for c in range(chunks)]
-        finish(0, y[0], res[0])
-        y.append(products(3, quantise(h_bf[3], P, "h3", 0)))
-        for c in range(1, chunks):
-            finish(c, y[c], res[c])
+        h_mx.append(quantise(h_bf[1][:], P, "h1", 512))
+        nc.vector.tensor_tensor(sums[:, 1, HALF:S], pair[:], g13b[:], ADD)
+        h_mx.append(quantise(h_bf[2][:], P, "h2", 1024))
+        finish(0)
+        h_mx.append(quantise(h_bf[3][:], P, "h3", 0))
+        for c in range(1, CHUNKS):
+            finish(c)

@@ -68,8 +68,9 @@ def tile_picked_ywide_none_p_kernel(tc, x_words, x_scales, w1, w2, wide, offs, c
         nc.vector.memset(scale_table[0:SCALE_ROW0, :].bitcast(I32), 0)
         zero = sb([P, 1], F32, "zero")
         nc.gpsimd.memset(zero[:], 0.0)
-        relu_bias = sb([P, 1], F32, "relu_bias")
-        nc.scalar.activation(relu_bias[:], zero[:], COPY)
+        shared = sb([P, 3 * HALF], F32, "shared")
+        relu_bias = shared[:, 0:1]
+        nc.scalar.activation(relu_bias, zero[:], COPY)
         x_sc = sb([P, S], U8, "x_sc")
         nc.gpsimd.memset(x_sc[:].bitcast(I32), 0)
 
@@ -117,30 +118,29 @@ def tile_picked_ywide_none_p_kernel(tc, x_words, x_scales, w1, w2, wide, offs, c
 
         g01 = look_up(True, sb([P, S], F32, "g01"), 0, list1, 0, S)
         g03 = look_up(False, sb([P, S], F32, "g03"), 0, list3, 0, S)
-        g02 = look_up(True, sb([P, P], F32, "g02a"), 0, list2, 0, P)
-        g02 = g02 + look_up(False, sb([P, S - P], F32, "g02b"), 0, list2, P, S - P)
+        g02 = look_up(True, sb([P, HALF], F32, "g02a"), 0, list2, 0, HALF)
+        g02 = g02 + look_up(False, sb([P, HALF], F32, "g02b"), 0, list2, HALF, HALF)
         g11b = sb([P, HALF], F32, "g11b")
         look_up(True, g11b, 1, list1, HALF, HALF)
-        g11a = look_up(True, sb([P, HALF], F32, "g11a"), 1, list1, 0, HALF)
         pair = sb([P, HALF], F32, "pair")
         nc.vector.tensor_tensor(pair[:], wide_rows[1][:].indirect(entries(list2, HALF, HALF)), g11b[:], ADD)
         g13a = look_up(False, sb([P, HALF], F32, "g13a"), 1, list3, 0, HALF)
-        g12a = look_up(False, placed([P, HALF], F32, "g12a", 16384), 1, list2, 0, HALF)
+        g12a = look_up(False, sb([P, HALF], F32, "g12a"), 1, list2, 0, HALF)
+        g11a = look_up(False, placed([P, HALF], F32, "g11a", 16384), 1, list1, 0, HALF)
 
-        shared = sb([P, 2 * S + HALF], F32, "shared")
-        sums = shared[:, 0 : 2 * S].rearrange("p (b n) -> p b n", b=2)
+        first_sums = sb([P, S], F32, "first_sums")
+        sums = [t[:, 0:S].rearrange("p (b n) -> p b n", b=2) for t in (first_sums, shared)]
         forth0 = turn(0, [g01, g03, g02])
-        forth1 = turn(2, [g11a, g13a, g12a])
+        forth1 = turn(2, [g13a, g12a, g11a])
         turned0 = sb([P, S], F32, "turned0")
         nc.scalar.activation(turned0[:], forth0, COPY)
         turned1 = sb([P, HALF], F32, "turned1")
         nc.scalar.activation(turned1[:], forth1, COPY)
         g13b = placed([P, HALF], F32, "g13b", 16384)
         look_up(False, g13b, 1, list3, HALF, HALF)
-        back0 = turn(1, [pieces(turned0, 4)])
-        back1 = turn(3, [pieces(turned1, 2)])
-        nc.scalar.activation(sums[:, 0, :], back0, COPY)
-        nc.scalar.activation(sums[:, 1, 0:HALF], back1, COPY)
+        back_late = turn(1, [pieces(turned0, 4)[2:4]])
+        back_first = turn(3, [pieces(turned0, 2) + pieces(turned1, 2)])
+        nc.scalar.activation(first_sums[:], back_first, COPY)
 
         w1_src = w1_raw[:].rearrange("p j (m t) -> p m j t", t=PACK)
         w1_bf = []
@@ -166,25 +166,26 @@ def tile_picked_ywide_none_p_kernel(tc, x_words, x_scales, w1, w2, wide, offs, c
                 h_bf[c][:].rearrange("p (n t) -> p n t", t=PACK),
                 bank[:].rearrange("p t n -> p n t"),
                 RELU,
-                bias=relu_bias[:],
+                bias=relu_bias,
             )
+        nc.scalar.activation(shared[:, 0:HALF], back_late, COPY)
 
-        w2_bf = shared[:, S + HALF : 2 * S + HALF].bitcast(BF16)
+        w2_bf = shared[:, HALF : 3 * HALF].bitcast(BF16)
         nc.vector.tensor_copy(w2_bf.rearrange("p (c i j) -> p c j i", i=4, j=PACK), w2_raw[:].rearrange("p j (c i) -> p c j i", i=4))
         h_mx = [quantise(h_bf[0][:], P, "h0", 0)]
         w2_mx = quantise(w2_bf, N, "w2")
         out_rows = out.rearrange("(b p) n -> p b n", p=P)
 
         def finish(c):
-            y = psum.tile([P, 2, P], F32, name="product%d" % c, tag="bank%d" % c)
+            y = psum.tile([P, 2, P], F32, name="product%d" % c, tag="bank%d" % [0, 2, 3, 4][c])
             for b in range(2):
                 product(y[:, b, :], w2_mx, slice(b * P, (b + 1) * P), h_mx[c], slice(0, P))
             res = sb([P, 2, P], F32, "res%d" % c)
-            nc.vector.tensor_tensor(res[:], y[:], sums[:, :, c * P : (c + 1) * P], ADD)
+            nc.vector.tensor_tensor(res[:], y[:], sums[c // 2][:, :, (c % 2) * P : (c % 2 + 1) * P], ADD)
             nc.sync.dma_start(out_rows[:, :, c * P : (c + 1) * P], res[:])
 
         h_mx.append(quantise(h_bf[1][:], P, "h1", 512))
-        nc.vector.tensor_tensor(sums[:, 1, HALF:S], pair[:], g13b[:], ADD)
+        nc.vector.tensor_tensor(shared[:, HALF:S], pair[:], g13b[:], ADD)
         h_mx.append(quantise(h_bf[2][:], P, "h2", 1024))
         finish(0)
         h_mx.append(quantise(h_bf[3][:], P, "h3", 0))

@@ -68,9 +68,9 @@ def tile_picked_ywide_none_p_kernel(tc, x_words, x_scales, w1, w2, wide, offs, c
         nc.vector.memset(scale_table[0:SCALE_ROW0, :].bitcast(I32), 0)
         zero = sb([P, 1], F32, "zero")
         nc.gpsimd.memset(zero[:], 0.0)
-        shared = sb([P, 3 * HALF], F32, "shared")
-        relu_bias = shared[:, 0:1]
-        nc.scalar.activation(relu_bias, zero[:], COPY)
+        shared = sb([P, S], F32, "shared")
+        relu_bias = sb([P, 1], F32, "relu_bias")
+        nc.scalar.activation(relu_bias[:], zero[:], COPY)
         x_sc = sb([P, S], U8, "x_sc")
         nc.gpsimd.memset(x_sc[:].bitcast(I32), 0)
 
@@ -97,7 +97,7 @@ def tile_picked_ywide_none_p_kernel(tc, x_words, x_scales, w1, w2, wide, offs, c
         def look_up(on_vector, dst, b, lst, first, count):
             window = wide_rows[b][:].indirect(entries(lst, first, count))
             if on_vector:
-                nc.vector.tensor_copy(dst[:], window)
+                nc.vector.tensor_copy(dst[:, :], window)
             else:
                 nc.scalar.activation(dst[:], window, COPY)
             return [dst[:, e * P : (e + 1) * P] for e in range(count // P)]
@@ -118,28 +118,35 @@ def tile_picked_ywide_none_p_kernel(tc, x_words, x_scales, w1, w2, wide, offs, c
 
         g01 = look_up(True, sb([P, S], F32, "g01"), 0, list1, 0, S)
         g03 = look_up(False, sb([P, S], F32, "g03"), 0, list3, 0, S)
-        g02 = look_up(True, sb([P, HALF], F32, "g02a"), 0, list2, 0, HALF)
-        g02 = g02 + look_up(False, sb([P, HALF], F32, "g02b"), 0, list2, HALF, HALF)
-        g11b = sb([P, HALF], F32, "g11b")
-        look_up(True, g11b, 1, list1, HALF, HALF)
+        g02 = look_up(True, sb([P, P], F32, "g02a"), 0, list2, 0, P)
+        g02 = g02 + look_up(False, sb([P, S - P], F32, "g02b"), 0, list2, P, S - P)
+        single = sb([P, HALF], F32, "single")
         pair = sb([P, HALF], F32, "pair")
-        nc.vector.tensor_tensor(pair[:], wide_rows[1][:].indirect(entries(list2, HALF, HALF)), g11b[:], ADD)
+        for e in range(2):
+            look_up(True, single[:, e * P : (e + 1) * P], 1, list1, HALF + e * P, P)
+        last_sums = shared[:].rearrange("p (e b n) -> p e b n", e=2, b=2)
+        for e in range(2):
+            cols = slice(e * P, (e + 1) * P)
+            nc.vector.tensor_tensor(pair[:, cols], wide_rows[1][:].indirect(entries(list2, HALF + e * P, P)), single[:, cols], ADD)
+        for e in range(2):
+            cols = slice(e * P, (e + 1) * P)
+            nc.vector.tensor_tensor(last_sums[:, e, 1, :], wide_rows[1][:].indirect(entries(list3, HALF + e * P, P)), pair[:, cols], ADD)
         g13a = look_up(False, sb([P, HALF], F32, "g13a"), 1, list3, 0, HALF)
         g12a = look_up(False, sb([P, HALF], F32, "g12a"), 1, list2, 0, HALF)
-        g11a = look_up(False, placed([P, HALF], F32, "g11a", 16384), 1, list1, 0, HALF)
+        g11a = look_up(False, sb([P, HALF], F32, "g11a"), 1, list1, 0, HALF)
 
         first_sums = sb([P, S], F32, "first_sums")
-        sums = [t[:, 0:S].rearrange("p (b n) -> p b n", b=2) for t in (first_sums, shared)]
+        by_block = first_sums[:].rearrange("p (b n) -> p b n", b=2)
+        sums = [by_block[:, :, 0:P], by_block[:, :, P:HALF], last_sums[:, 0], last_sums[:, 1]]
         forth0 = turn(0, [g01, g03, g02])
         forth1 = turn(2, [g13a, g12a, g11a])
         turned0 = sb([P, S], F32, "turned0")
         nc.scalar.activation(turned0[:], forth0, COPY)
         turned1 = sb([P, HALF], F32, "turned1")
         nc.scalar.activation(turned1[:], forth1, COPY)
-        g13b = placed([P, HALF], F32, "g13b", 16384)
-        look_up(False, g13b, 1, list3, HALF, HALF)
-        back_late = turn(1, [pieces(turned0, 4)[2:4]])
+        back_second = turn(1, [pieces(turned0, 4)[2:4]])
         back_first = turn(3, [pieces(turned0, 2) + pieces(turned1, 2)])
+        nc.scalar.activation(last_sums[:, :, 0, :], back_second.rearrange("p (e n) -> p e n", e=2), COPY)
         nc.scalar.activation(first_sums[:], back_first, COPY)
 
         w1_src = w1_raw[:].rearrange("p j (m t) -> p m j t", t=PACK)
@@ -166,28 +173,31 @@ def tile_picked_ywide_none_p_kernel(tc, x_words, x_scales, w1, w2, wide, offs, c
                 h_bf[c][:].rearrange("p (n t) -> p n t", t=PACK),
                 bank[:].rearrange("p t n -> p n t"),
                 RELU,
-                bias=relu_bias,
+                bias=relu_bias[:],
             )
-        nc.scalar.activation(shared[:, 0:HALF], back_late, COPY)
 
-        w2_bf = shared[:, HALF : 3 * HALF].bitcast(BF16)
-        nc.vector.tensor_copy(w2_bf.rearrange("p (c i j) -> p c j i", i=4, j=PACK), w2_raw[:].rearrange("p j (c i) -> p c j i", i=4))
-        h_mx = [quantise(h_bf[0][:], P, "h0", 0)]
-        w2_mx = quantise(w2_bf, N, "w2")
+        w2_bf = []
+        for b in range(2):
+            t = sb([P, P * PACK], BF16, "w2_bf%d" % b)
+            nc.vector.tensor_copy(
+                t[:].rearrange("p (c i j) -> p c j i", i=4, j=PACK),
+                w2_raw[:, :, b * P : (b + 1) * P].rearrange("p j (c i) -> p c j i", i=4),
+            )
+            w2_bf.append(t)
+        w2_mx = [quantise(w2_bf[b][:], P, "w2_%d" % b) for b in range(2)]
+        h_mx = [quantise(h_bf[c][:], P, "h%d" % c, 512 * c) for c in range(2)]
         out_rows = out.rearrange("(b p) n -> p b n", p=P)
 
         def finish(c):
             y = psum.tile([P, 2, P], F32, name="product%d" % c, tag="bank%d" % [0, 2, 3, 4][c])
             for b in range(2):
-                product(y[:, b, :], w2_mx, slice(b * P, (b + 1) * P), h_mx[c], slice(0, P))
-            res = sb([P, 2, P], F32, "res%d" % c)
-            nc.vector.tensor_tensor(res[:], y[:], sums[c // 2][:, :, (c % 2) * P : (c % 2 + 1) * P], ADD)
-            nc.sync.dma_start(out_rows[:, :, c * P : (c + 1) * P], res[:])
+                product(y[:, b, :], w2_mx[b], slice(0, P), h_mx[c], slice(0, P))
+            for blocks in [slice(0, 2)] if c + 1 < CHUNKS else [slice(0, 1), slice(1, 2)]:
+                res = sb([P, blocks.stop - blocks.start, P], F32, "res%d_%d" % (c, blocks.start))
+                nc.vector.tensor_tensor(res[:], y[:, blocks, :], sums[c][:, blocks, :], ADD)
+                nc.sync.dma_start(out_rows[:, blocks, c * P : (c + 1) * P], res[:])
 
-        h_mx.append(quantise(h_bf[1][:], P, "h1", 512))
-        nc.vector.tensor_tensor(shared[:, HALF:S], pair[:], g13b[:], ADD)
-        h_mx.append(quantise(h_bf[2][:], P, "h2", 1024))
-        finish(0)
-        h_mx.append(quantise(h_bf[3][:], P, "h3", 0))
-        for c in range(1, CHUNKS):
+        for c in range(CHUNKS):
             finish(c)
+            if c + 2 < CHUNKS:
+                h_mx.append(quantise(h_bf[c + 2][:], P, "h%d" % (c + 2), 512 * c))

@@ -32,10 +32,10 @@ def tile_picked_ywide_none_p_kernel(tc, x_words, x_scales, w1, w2, wide, offs, c
         psum = ctx.enter_context(tc.psum_pool(name="psum", bufs=1))
 
         def sb(shape, dtype, name):
-            return keep.tile(shape, dtype, name=name, align_bytes=64)
+            return keep.tile(shape, dtype, name=name, align_bytes=256)
 
         def placed(shape, dtype, name, offset):
-            return reuse.tile(shape, dtype, name=name, align_bytes=64, offset=offset)
+            return reuse.tile(shape, dtype, name=name, align_bytes=256, offset=offset)
 
         def load_list(src, name):
             t = keep.tile([P, S // 16], U16, name=name)

@@ -68,7 +68,6 @@ def tile_picked_ywide_none_p_kernel(tc, x_words, x_scales, w1, w2, wide, offs, c
         nc.vector.memset(scale_table[0:SCALE_ROW0, :].bitcast(I32), 0)
         zero = sb([P, 1], F32, "zero")
         nc.gpsimd.memset(zero[:], 0.0)
-        shared = sb([P, S], F32, "shared")
         relu_bias = sb([P, 1], F32, "relu_bias")
         nc.scalar.activation(relu_bias[:], zero[:], COPY)
         x_sc = sb([P, S], U8, "x_sc")
@@ -120,24 +119,17 @@ def tile_picked_ywide_none_p_kernel(tc, x_words, x_scales, w1, w2, wide, offs, c
         g03 = look_up(False, sb([P, S], F32, "g03"), 0, list3, 0, S)
         g02 = look_up(True, sb([P, P], F32, "g02a"), 0, list2, 0, P)
         g02 = g02 + look_up(False, sb([P, S - P], F32, "g02b"), 0, list2, P, S - P)
-        single = sb([P, HALF], F32, "single")
+        late = [sb([P, HALF], F32, "late%d" % k) for k in range(3)]
+        for k, lst in enumerate([list1, list2, list3]):
+            look_up(True, late[k], 1, lst, HALF, HALF)
         pair = sb([P, HALF], F32, "pair")
-        for e in range(2):
-            look_up(True, single[:, e * P : (e + 1) * P], 1, list1, HALF + e * P, P)
-        last_sums = shared[:].rearrange("p (e b n) -> p e b n", e=2, b=2)
-        for e in range(2):
-            cols = slice(e * P, (e + 1) * P)
-            nc.vector.tensor_tensor(pair[:, cols], wide_rows[1][:].indirect(entries(list2, HALF + e * P, P)), single[:, cols], ADD)
-        for e in range(2):
-            cols = slice(e * P, (e + 1) * P)
-            nc.vector.tensor_tensor(last_sums[:, e, 1, :], wide_rows[1][:].indirect(entries(list3, HALF + e * P, P)), pair[:, cols], ADD)
+        nc.gpsimd.tensor_tensor(pair[:], late[0][:], late[1][:], ADD)
         g13a = look_up(False, sb([P, HALF], F32, "g13a"), 1, list3, 0, HALF)
         g12a = look_up(False, sb([P, HALF], F32, "g12a"), 1, list2, 0, HALF)
         g11a = look_up(False, sb([P, HALF], F32, "g11a"), 1, list1, 0, HALF)
 
         first_sums = sb([P, S], F32, "first_sums")
         by_block = first_sums[:].rearrange("p (b n) -> p b n", b=2)
-        sums = [by_block[:, :, 0:P], by_block[:, :, P:HALF], last_sums[:, 0], last_sums[:, 1]]
         forth0 = turn(0, [g01, g03, g02])
         forth1 = turn(2, [g13a, g12a, g11a])
         turned0 = sb([P, S], F32, "turned0")
@@ -146,16 +138,21 @@ def tile_picked_ywide_none_p_kernel(tc, x_words, x_scales, w1, w2, wide, offs, c
         nc.scalar.activation(turned1[:], forth1, COPY)
         back_second = turn(1, [pieces(turned0, 4)[2:4]])
         back_first = turn(3, [pieces(turned0, 2) + pieces(turned1, 2)])
-        nc.scalar.activation(last_sums[:, :, 0, :], back_second.rearrange("p (e n) -> p e n", e=2), COPY)
-        nc.scalar.activation(first_sums[:], back_first, COPY)
 
         w1_src = w1_raw[:].rearrange("p j (m t) -> p m j t", t=PACK)
         w1_bf = []
         for u in range(2):
-            t = sb([P, 2 * P * PACK], BF16, "w1_bf%d" % u)
+            t = placed([P, 2 * P * PACK], BF16, "w1_bf%d" % u, 12288 + 2048 * u)
             nc.vector.tensor_copy(t[:].rearrange("p (t m j) -> p m j t", t=2, j=PACK), w1_src[:, :, :, 2 * u : 2 * u + 2])
             w1_bf.append(t)
         w1_mx = [quantise(w1_bf[u][:], 2 * P, "w1_%d" % u) for u in range(2)]
+
+        last_sums = placed([P, 2, 2, P], F32, "last_sums", 12288 + 2048)
+        by_group = [t[:].rearrange("p (e n) -> p e n", e=2) for t in [pair, late[2]]]
+        nc.gpsimd.tensor_tensor(last_sums[:, :, 1, :], by_group[0], by_group[1], ADD)
+        nc.scalar.activation(last_sums[:, :, 0, :], back_second.rearrange("p (e n) -> p e n", e=2), COPY)
+        nc.scalar.activation(first_sums[:], back_first, COPY)
+        sums = [by_block[:, :, 0:P], by_block[:, :, P:HALF], last_sums[:, 0], last_sums[:, 1]]
 
         x_codes = []
         for first, width in [(0, P), (P, P), (HALF, HALF)]:

@@ -12,6 +12,7 @@ U8 = mybir.dt.uint8
 FP8X4 = mybir.dt.float8_e4m3fn_x4
 ADD = mybir.AluOpType.add
 COPY = mybir.ActivationFunctionType.Copy
+IDENTITY = mybir.ActivationFunctionType.Identity
 RELU = mybir.ActivationFunctionType.Relu
 
 K, T, S, H, N, R = 512, 2048, 512, 512, 256, 1024
@@ -68,8 +69,8 @@ def tile_picked_ywide_none_p_kernel(tc, x_words, x_scales, w1, w2, wide, offs, c
         nc.vector.memset(scale_table[0:SCALE_ROW0, :].bitcast(I32), 0)
         zero = sb([P, 1], F32, "zero")
         nc.gpsimd.memset(zero[:], 0.0)
-        relu_bias = sb([P, 1], F32, "relu_bias")
-        nc.scalar.activation(relu_bias[:], zero[:], COPY)
+        zero_bias = sb([P, 1], F32, "zero_bias")
+        nc.scalar.activation(zero_bias[:], zero[:], COPY)
         x_sc = sb([P, S], U8, "x_sc")
         nc.gpsimd.memset(x_sc[:].bitcast(I32), 0)
 
@@ -133,7 +134,7 @@ def tile_picked_ywide_none_p_kernel(tc, x_words, x_scales, w1, w2, wide, offs, c
         forth0 = turn(0, [g01, g03, g02])
         forth1 = turn(2, [g13a, g12a, g11a])
         turned0 = sb([P, S], F32, "turned0")
-        nc.scalar.activation(turned0[:], forth0, COPY)
+        nc.scalar.activation(turned0[:], forth0, IDENTITY, bias=zero_bias[:])
         turned1 = sb([P, HALF], F32, "turned1")
         nc.scalar.activation(turned1[:], forth1, COPY)
         back_second = turn(1, [pieces(turned0, 4)[2:4]])
@@ -170,7 +171,6 @@ def tile_picked_ywide_none_p_kernel(tc, x_words, x_scales, w1, w2, wide, offs, c
                 h_bf[c][:].rearrange("p (n t) -> p n t", t=PACK),
                 bank[:].rearrange("p t n -> p n t"),
                 RELU,
-                bias=relu_bias[:],
             )
 
         w2_bf = []
@@ -185,16 +185,18 @@ def tile_picked_ywide_none_p_kernel(tc, x_words, x_scales, w1, w2, wide, offs, c
         h_mx = [quantise(h_bf[c][:], P, "h%d" % c, 512 * c) for c in range(2)]
         out_rows = out.rearrange("(b p) n -> p b n", p=P)
 
-        def finish(c):
-            y = psum.tile([P, 2, P], F32, name="product%d" % c, tag="bank%d" % [0, 2, 3, 4][c])
-            for b in range(2):
-                product(y[:, b, :], w2_mx[b], slice(0, P), h_mx[c], slice(0, P))
-            for blocks in [slice(0, 2)] if c + 1 < CHUNKS else [slice(0, 1), slice(1, 2)]:
-                res = sb([P, blocks.stop - blocks.start, P], F32, "res%d_%d" % (c, blocks.start))
-                nc.vector.tensor_tensor(res[:], y[:, blocks, :], sums[c][:, blocks, :], ADD)
-                nc.sync.dma_start(out_rows[:, blocks, c * P : (c + 1) * P], res[:])
+        def finish(c, blocks, bank):
+            count = blocks.stop - blocks.start
+            y = psum.tile([P, count, P], F32, name="product%d_%d" % (c, blocks.start), tag="bank%d" % bank)
+            for b in range(count):
+                product(y[:, b, :], w2_mx[blocks.start + b], slice(0, P), h_mx[c], slice(0, P))
+            res = sb([P, count, P], F32, "res%d_%d" % (c, blocks.start))
+            nc.vector.tensor_tensor(res[:], y[:], sums[c][:, blocks, :], ADD)
+            nc.sync.dma_start(out_rows[:, blocks, c * P : (c + 1) * P], res[:])
 
-        for c in range(CHUNKS):
-            finish(c)
+        for c, bank in enumerate([0, 2, 3]):
+            finish(c, slice(0, 2), bank)
             if c + 2 < CHUNKS:
                 h_mx.append(quantise(h_bf[c + 2][:], P, "h%d" % (c + 2), 512 * c))
+        for b, bank in enumerate([4, 1]):
+            finish(CHUNKS - 1, slice(b, b + 1), bank)

@@ -12,7 +12,6 @@ U8 = mybir.dt.uint8
 FP8X4 = mybir.dt.float8_e4m3fn_x4
 ADD = mybir.AluOpType.add
 COPY = mybir.ActivationFunctionType.Copy
-IDENTITY = mybir.ActivationFunctionType.Identity
 RELU = mybir.ActivationFunctionType.Relu
 
 K, T, S, H, N, R = 512, 2048, 512, 512, 256, 1024
@@ -69,7 +68,7 @@ def tile_picked_ywide_none_p_kernel(tc, x_words, x_scales, w1, w2, wide, offs, c
         nc.vector.memset(scale_table[0:SCALE_ROW0, :].bitcast(I32), 0)
         zero = sb([P, 1], F32, "zero")
         nc.gpsimd.memset(zero[:], 0.0)
-        zero_bias = sb([P, 1], F32, "zero_bias")
+        zero_bias = placed([P, 1], F32, "zero_bias", 16384)
         nc.scalar.activation(zero_bias[:], zero[:], COPY)
         x_sc = sb([P, S], U8, "x_sc")
         nc.gpsimd.memset(x_sc[:].bitcast(I32), 0)
@@ -134,7 +133,7 @@ def tile_picked_ywide_none_p_kernel(tc, x_words, x_scales, w1, w2, wide, offs, c
         forth0 = turn(0, [g01, g03, g02])
         forth1 = turn(2, [g13a, g12a, g11a])
         turned0 = sb([P, S], F32, "turned0")
-        nc.scalar.activation(turned0[:], forth0, IDENTITY, bias=zero_bias[:])
+        nc.scalar.activation(turned0[:], forth0, COPY)
         turned1 = sb([P, HALF], F32, "turned1")
         nc.scalar.activation(turned1[:], forth1, COPY)
         back_second = turn(1, [pieces(turned0, 4)[2:4]])
@@ -171,6 +170,7 @@ def tile_picked_ywide_none_p_kernel(tc, x_words, x_scales, w1, w2, wide, offs, c
                 h_bf[c][:].rearrange("p (n t) -> p n t", t=PACK),
                 bank[:].rearrange("p t n -> p n t"),
                 RELU,
+                bias=zero_bias[:] if c == 2 else 0.0,
             )
 
         w2_bf = []
@@ -185,18 +185,20 @@ def tile_picked_ywide_none_p_kernel(tc, x_words, x_scales, w1, w2, wide, offs, c
         h_mx = [quantise(h_bf[c][:], P, "h%d" % c, 512 * c) for c in range(2)]
         out_rows = out.rearrange("(b p) n -> p b n", p=P)
 
-        def finish(c, blocks, bank):
+        def finish(c, blocks, bank, offset=None):
             count = blocks.stop - blocks.start
             y = psum.tile([P, count, P], F32, name="product%d_%d" % (c, blocks.start), tag="bank%d" % bank)
             for b in range(count):
                 product(y[:, b, :], w2_mx[blocks.start + b], slice(0, P), h_mx[c], slice(0, P))
-            res = sb([P, count, P], F32, "res%d_%d" % (c, blocks.start))
+            name = "res%d_%d" % (c, blocks.start)
+            res = sb([P, count, P], F32, name) if offset is None else placed([P, count, P], F32, name, offset)
             nc.vector.tensor_tensor(res[:], y[:], sums[c][:, blocks, :], ADD)
             nc.sync.dma_start(out_rows[:, blocks, c * P : (c + 1) * P], res[:])
 
-        for c, bank in enumerate([0, 2, 3]):
-            finish(c, slice(0, 2), bank)
-            if c + 2 < CHUNKS:
-                h_mx.append(quantise(h_bf[c + 2][:], P, "h%d" % (c + 2), 512 * c))
+        h_mx.append(quantise(h_bf[2][:], P, "h2"))
+        finish(0, slice(0, 2), 0, 16384)
+        h_mx.append(quantise(h_bf[3][:], P, "h3", 0))
+        finish(1, slice(0, 2), 2)
+        finish(2, slice(0, 2), 3)
         for b, bank in enumerate([4, 1]):
             finish(CHUNKS - 1, slice(b, b + 1), bank)

@@ -62,7 +62,7 @@ def tile_picked_ywide_none_p_kernel(tc, x_words, x_scales, w1, w2, wide, offs, c
                 stop=True,
             )
 
-        scale_table = placed([P, T], U8, "scale_table", 3072)
+        scale_table = placed([P, T], U8, "scale_table", 2048)
         nc.scalar.dma_start(scale_table[SCALE_ROW0:P, :].bitcast(I32), x_scales[0].bitcast(I32))
         users = load_list(offs, "users")
         nc.vector.memset(scale_table[0:SCALE_ROW0, :].bitcast(I32), 0)
@@ -84,12 +84,12 @@ def tile_picked_ywide_none_p_kernel(tc, x_words, x_scales, w1, w2, wide, offs, c
         nc.sync.dma_start(wide_rows[1][:], wide[P : 2 * P, :])
         w1_raw = sb([P, PACK, H], F32, "w1_raw")
         nc.sync.dma_start(w1_raw[:], w1.rearrange("(p j) c -> p j c", j=PACK))
+        word_table = placed([P, T], I32, "word_table", 4096)
+        nc.sync.dma_start(word_table[:], x_words[0].rearrange("p n t -> p (n t)").bitcast(I32))
         sc_picked = sb([P, S], U8, "sc_picked")
         nc.vector.tensor_copy(sc_picked[:], scale_table[:].indirect(users[:]))
         for r in range(4):
             nc.sync.dma_start(x_sc[r:P:32, :].bitcast(I32), sc_picked[SCALE_ROW0 + r : P : 4, :].bitcast(I32))
-        word_table = placed([P, T], I32, "word_table", 4096)
-        nc.sync.dma_start(word_table[:], x_words[0].rearrange("p n t -> p (n t)").bitcast(I32))
         w2_raw = placed([P, PACK, N], F32, "w2_raw", 0)
         nc.sync.dma_start(w2_raw[:], w2.rearrange("(p j) c -> p j c", j=PACK))
 
@@ -185,7 +185,7 @@ def tile_picked_ywide_none_p_kernel(tc, x_words, x_scales, w1, w2, wide, offs, c
         h_mx = [quantise(h_bf[c][:], P, "h%d" % c, 512 * c) for c in range(2)]
         out_rows = out.rearrange("(b p) n -> p b n", p=P)
 
-        def finish(c, blocks, bank, offset=None):
+        def finish(c, blocks, bank, offset=None, queue=nc.sync):
             count = blocks.stop - blocks.start
             y = psum.tile([P, count, P], F32, name="product%d_%d" % (c, blocks.start), tag="bank%d" % bank)
             for b in range(count):
@@ -193,12 +193,12 @@ def tile_picked_ywide_none_p_kernel(tc, x_words, x_scales, w1, w2, wide, offs, c
             name = "res%d_%d" % (c, blocks.start)
             res = sb([P, count, P], F32, name) if offset is None else placed([P, count, P], F32, name, offset)
             nc.vector.tensor_tensor(res[:], y[:], sums[c][:, blocks, :], ADD)
-            nc.sync.dma_start(out_rows[:, blocks, c * P : (c + 1) * P], res[:])
+            queue.dma_start(out_rows[:, blocks, c * P : (c + 1) * P], res[:])
 
         h_mx.append(quantise(h_bf[2][:], P, "h2"))
         finish(0, slice(0, 2), 0, 16384)
         h_mx.append(quantise(h_bf[3][:], P, "h3", 0))
         finish(1, slice(0, 2), 2)
         finish(2, slice(0, 2), 3)
-        for b, bank in enumerate([4, 1]):
-            finish(CHUNKS - 1, slice(b, b + 1), bank)
+        finish(CHUNKS - 1, slice(0, 1), 4, queue=nc.scalar)
+        finish(CHUNKS - 1, slice(1, 2), 1)

@@ -185,7 +185,7 @@ def tile_picked_ywide_none_p_kernel(tc, x_words, x_scales, w1, w2, wide, offs, c
         h_mx = [quantise(h_bf[c][:], P, "h%d" % c, 512 * c) for c in range(2)]
         out_rows = out.rearrange("(b p) n -> p b n", p=P)
 
-        def finish(c, blocks, bank, offset=None, queue=nc.sync):
+        def finish(c, blocks, bank, offset=None):
             count = blocks.stop - blocks.start
             y = psum.tile([P, count, P], F32, name="product%d_%d" % (c, blocks.start), tag="bank%d" % bank)
             for b in range(count):
@@ -193,12 +193,12 @@ def tile_picked_ywide_none_p_kernel(tc, x_words, x_scales, w1, w2, wide, offs, c
             name = "res%d_%d" % (c, blocks.start)
             res = sb([P, count, P], F32, name) if offset is None else placed([P, count, P], F32, name, offset)
             nc.vector.tensor_tensor(res[:], y[:], sums[c][:, blocks, :], ADD)
-            queue.dma_start(out_rows[:, blocks, c * P : (c + 1) * P], res[:])
+            nc.sync.dma_start(out_rows[:, blocks, c * P : (c + 1) * P], res[:])
 
         h_mx.append(quantise(h_bf[2][:], P, "h2"))
         finish(0, slice(0, 2), 0, 16384)
         h_mx.append(quantise(h_bf[3][:], P, "h3", 0))
         finish(1, slice(0, 2), 2)
         finish(2, slice(0, 2), 3)
-        finish(CHUNKS - 1, slice(0, 1), 4, queue=nc.scalar)
-        finish(CHUNKS - 1, slice(1, 2), 1)
+        for b, bank in enumerate([4, 1]):
+            finish(CHUNKS - 1, slice(b, b + 1), bank)

from contextlib import ExitStack

import concourse.mybir as mybir
from concourse.masks import make_identity

F32 = mybir.dt.float32
BF16 = mybir.dt.bfloat16
I32 = mybir.dt.int32
U32 = mybir.dt.uint32
U16 = mybir.dt.uint16
U8 = mybir.dt.uint8
FP8X4 = mybir.dt.float8_e4m3fn_x4
ADD = mybir.AluOpType.add
COPY = mybir.ActivationFunctionType.Copy
RELU = mybir.ActivationFunctionType.Relu

K, T, S, H, N, R = 512, 2048, 512, 512, 256, 1024
P = 128
PACK = 4
BLOCKS = K // 32
SCALE_ROW0 = P - BLOCKS
HALF = S // 2
CHUNKS = S // P
FLOPS = 2 * K * H * S + 2 * H * N * S


def tile_picked_ywide_none_p_kernel(tc, x_words, x_scales, w1, w2, wide, offs, cross1, cross2, cross3, out):
    nc = tc.nc
    with ExitStack() as ctx:
        keep = ctx.enter_context(tc.tile_pool(name="keep", bufs=1))
        reuse = ctx.enter_context(tc.tile_pool(name="reuse", bufs=1))
        psum = ctx.enter_context(tc.psum_pool(name="psum", bufs=1))

        def sb(shape, dtype, name):
            return keep.tile(shape, dtype, name=name, align_bytes=256)

        def placed(shape, dtype, name, offset):
            return reuse.tile(shape, dtype, name=name, align_bytes=256, offset=offset)

        def load_list(src, name):
            t = keep.tile([P, S // 16], U16, name=name)
            nc.sync.dma_start(t[:], src)
            return t

        def entries(lst, first, count):
            return lst[:, first // 16 : (first + count) // 16]

        def quantise(src, width, name, offset=None):
            codes = sb([P, width], U32, name + "_codes") if offset is None else placed([P, width], U32, name + "_codes", offset)
            scales = sb([P, width], U8, name + "_sc")
            nc.vector.quantize_mx(out=codes[:].bitcast(FP8X4), scales=scales[:], in_=src)
            return codes, scales

        def product(dst, lhs, lcols, rhs, rcols):
            nc.tensor.matmul_mx(
                out=dst,
                lhsT=lhs[0][:, lcols].bitcast(FP8X4),
                lhsT_scale=lhs[1][:, lcols],
                rhs=rhs[0][:, rcols].bitcast(FP8X4),
                rhs_scale=rhs[1][:, rcols],
                start=True,
                stop=True,
            )

        scale_table = placed([P, T], U8, "scale_table", 2048)
        nc.scalar.dma_start(scale_table[SCALE_ROW0:P, :].bitcast(I32), x_scales[0].bitcast(I32))
        users = load_list(offs, "users")
        nc.vector.memset(scale_table[0:SCALE_ROW0, :].bitcast(I32), 0)
        zero = sb([P, 1], F32, "zero")
        nc.gpsimd.memset(zero[:], 0.0)
        zero_bias = placed([P, 1], F32, "zero_bias", 16384)
        nc.scalar.activation(zero_bias[:], zero[:], COPY)
        x_sc = sb([P, S], U8, "x_sc")
        nc.gpsimd.memset(x_sc[:].bitcast(I32), 0)

        ident = sb([P, P], F32, "ident")
        make_identity(nc, ident[:])

        wide_rows = [sb([P, R], F32, "wide%d" % b) for b in range(2)]
        nc.sync.dma_start(wide_rows[0][:], wide[0:P, :])
        list1 = load_list(cross1, "list1")
        list3 = load_list(cross3, "list3")
        list2 = load_list(cross2, "list2")
        nc.sync.dma_start(wide_rows[1][:], wide[P : 2 * P, :])
        w1_raw = sb([P, PACK, H], F32, "w1_raw")
        nc.sync.dma_start(w1_raw[:], w1.rearrange("(p j) c -> p j c", j=PACK))
        word_table = placed([P, T], I32, "word_table", 4096)
        nc.sync.dma_start(word_table[:], x_words[0].rearrange("p n t -> p (n t)").bitcast(I32))
        sc_picked = sb([P, S], U8, "sc_picked")
        nc.vector.tensor_copy(sc_picked[:], scale_table[:].indirect(users[:]))
        for r in range(4):
            nc.sync.dma_start(x_sc[r:P:32, :].bitcast(I32), sc_picked[SCALE_ROW0 + r : P : 4, :].bitcast(I32))
        w2_raw = placed([P, PACK, N], F32, "w2_raw", 0)
        nc.sync.dma_start(w2_raw[:], w2.rearrange("(p j) c -> p j c", j=PACK))

        def look_up(on_vector, dst, b, lst, first, count):
            window = wide_rows[b][:].indirect(entries(lst, first, count))
            if on_vector:
                nc.vector.tensor_copy(dst[:, :], window)
            else:
                nc.scalar.activation(dst[:], window, COPY)
            return [dst[:, e * P : (e + 1) * P] for e in range(count // P)]

        def turn(bank, sources):
            count = len(sources[0])
            dst = psum.tile([P, count, P], F32, name="turn%d" % bank, tag="bank%d" % bank)
            for k, src in enumerate(sources):
                for e in range(count):
                    nc.tensor.matmul(
                        dst[:, e, :], src[e], ident[:],
                        start=(k == 0 and e == 0), stop=(k == len(sources) - 1 and e == count - 1), is_transpose=True,
                    )
            return dst[:].rearrange("p e n -> p (e n)")

        def pieces(t, count):
            return [t[:, e * P : (e + 1) * P] for e in range(count)]

        g01 = look_up(True, sb([P, S], F32, "g01"), 0, list1, 0, S)
        g03 = look_up(False, sb([P, S], F32, "g03"), 0, list3, 0, S)
        g02 = look_up(True, sb([P, P], F32, "g02a"), 0, list2, 0, P)
        g02 = g02 + look_up(False, sb([P, S - P], F32, "g02b"), 0, list2, P, S - P)
        late = [sb([P, HALF], F32, "late%d" % k) for k in range(3)]
        for k, lst in enumerate([list1, list2, list3]):
            look_up(True, late[k], 1, lst, HALF, HALF)
        pair = sb([P, HALF], F32, "pair")
        nc.gpsimd.tensor_tensor(pair[:], late[0][:], late[1][:], ADD)
        g13a = look_up(False, sb([P, HALF], F32, "g13a"), 1, list3, 0, HALF)
        g12a = look_up(False, sb([P, HALF], F32, "g12a"), 1, list2, 0, HALF)
        g11a = look_up(False, sb([P, HALF], F32, "g11a"), 1, list1, 0, HALF)

        first_sums = sb([P, S], F32, "first_sums")
        by_block = first_sums[:].rearrange("p (b n) -> p b n", b=2)
        forth0 = turn(0, [g01, g03, g02])
        forth1 = turn(2, [g13a, g12a, g11a])
        turned0 = sb([P, S], F32, "turned0")
        nc.scalar.activation(turned0[:], forth0, COPY)
        turned1 = sb([P, HALF], F32, "turned1")
        nc.scalar.activation(turned1[:], forth1, COPY)
        back_second = turn(1, [pieces(turned0, 4)[2:4]])
        back_first = turn(3, [pieces(turned0, 2) + pieces(turned1, 2)])

        w1_src = w1_raw[:].rearrange("p j (m t) -> p m j t", t=PACK)
        w1_bf = []
        for u in range(2):
            t = placed([P, 2 * P * PACK], BF16, "w1_bf%d" % u, 12288 + 2048 * u)
            nc.vector.tensor_copy(t[:].rearrange("p (t m j) -> p m j t", t=2, j=PACK), w1_src[:, :, :, 2 * u : 2 * u + 2])
            w1_bf.append(t)
        w1_mx = [quantise(w1_bf[u][:], 2 * P, "w1_%d" % u) for u in range(2)]

        last_sums = placed([P, 2, 2, P], F32, "last_sums", 12288 + 2048)
        by_group = [t[:].rearrange("p (e n) -> p e n", e=2) for t in [pair, late[2]]]
        nc.gpsimd.tensor_tensor(last_sums[:, :, 1, :], by_group[0], by_group[1], ADD)
        nc.scalar.activation(last_sums[:, :, 0, :], back_second.rearrange("p (e n) -> p e n", e=2), COPY)
        nc.scalar.activation(first_sums[:], back_first, COPY)
        sums = [by_block[:, :, 0:P], by_block[:, :, P:HALF], last_sums[:, 0], last_sums[:, 1]]

        x_codes = []
        for first, width in [(0, P), (P, P), (HALF, HALF)]:
            picked = sb([P, width], U32, "x_codes%d" % first)
            nc.vector.tensor_copy(picked[:], word_table[:].bitcast(U32).indirect(entries(users, first, width)))
            x_codes.extend(picked[:, e * P : (e + 1) * P] for e in range(width // P))

        h_bf = [sb([P, P * PACK], BF16, "h_bf%d" % c) for c in range(CHUNKS)]
        for c in range(CHUNKS):
            bank = psum.tile([P, PACK, P], F32, name="hidden%d" % c, tag="bank%d" % (4 + c))
            for t in range(PACK):
                u, e = divmod(t, 2)
                product(bank[:, t, :], w1_mx[u], slice(e * P, (e + 1) * P), (x_codes[c], x_sc[:, c * P : (c + 1) * P]), slice(0, P))
            nc.scalar.activation(
                h_bf[c][:].rearrange("p (n t) -> p n t", t=PACK),
                bank[:].rearrange("p t n -> p n t"),
                RELU,
                bias=zero_bias[:] if c == 2 else 0.0,
            )

        w2_bf = []
        for b in range(2):
            t = sb([P, P * PACK], BF16, "w2_bf%d" % b)
            nc.vector.tensor_copy(
                t[:].rearrange("p (c i j) -> p c j i", i=4, j=PACK),
                w2_raw[:, :, b * P : (b + 1) * P].rearrange("p j (c i) -> p c j i", i=4),
            )
            w2_bf.append(t)
        w2_mx = [quantise(w2_bf[b][:], P, "w2_%d" % b) for b in range(2)]
        h_mx = [quantise(h_bf[c][:], P, "h%d" % c, 512 * c) for c in range(2)]
        out_rows = out.rearrange("(b p) n -> p b n", p=P)

        def finish(c, blocks, bank, offset=None):
            count = blocks.stop - blocks.start
            y = psum.tile([P, count, P], F32, name="product%d_%d" % (c, blocks.start), tag="bank%d" % bank)
            for b in range(count):
                product(y[:, b, :], w2_mx[blocks.start + b], slice(0, P), h_mx[c], slice(0, P))
            name = "res%d_%d" % (c, blocks.start)
            res = sb([P, count, P], F32, name) if offset is None else placed([P, count, P], F32, name, offset)
            nc.vector.tensor_tensor(res[:], y[:], sums[c][:, blocks, :], ADD)
            nc.sync.dma_start(out_rows[:, blocks, c * P : (c + 1) * P], res[:])

        h_mx.append(quantise(h_bf[2][:], P, "h2"))
        finish(0, slice(0, 2), 0, 16384)
        h_mx.append(quantise(h_bf[3][:], P, "h3", 0))
        finish(1, slice(0, 2), 2)
        finish(2, slice(0, 2), 3)
        for b, bank in enumerate([4, 1]):
            finish(CHUNKS - 1, slice(b, b + 1), bank)
